import numpy as np
import ml_dtypes


def mxq(x, axis, fmt="e4m3"):
    dtype, down = {"e4m3": (ml_dtypes.float8_e4m3fn, 7), "e5m2": (ml_dtypes.float8_e5m2, 14)}[fmt]
    v = np.moveaxis(np.asarray(x, np.float32).astype(ml_dtypes.bfloat16).astype(np.float64), axis, -1)
    blocks = v.reshape(v.shape[:-1] + (-1, 32))
    amax = np.abs(blocks).max(-1, keepdims=True)
    byte = np.maximum(np.where(amax > 0, np.frexp(amax)[1] - 1 + 127, 0) - down, 1)
    scale = np.exp2(byte - 127.0)
    codes = (blocks / scale).astype(np.float32).astype(dtype).astype(np.float64)
    return np.moveaxis((codes * scale).reshape(v.shape), -1, axis)


WIDE = False


def mx_kscale(k):
    if not WIDE:
        return np.ones(k)
    levels = np.array([10, -10, 5, -5, 0])
    if k % 512:
        return np.exp2(np.random.permutation(np.resize(levels, k // 32))).repeat(32)
    a = np.empty((k // 512, 16))
    for p in range(k // 512):
        a[p, :8] = np.random.permutation(np.resize(levels, 8))
        for g in range(8):
            far = levels[np.abs(levels - a[p, g]) >= 10]
            a[p, g + 8] = far[np.random.randint(len(far))]
    return np.exp2(a.ravel()).repeat(32)


def f64(x):
    return np.asarray(x).astype(np.float64)


def striped(idx):
    return np.tile(idx.reshape(-1, 16).T, (8, 1)).astype(np.uint16)


def unstriped(offs):
    return offs[:16].T.reshape(-1).astype(np.int64)


def pack_weight(w):
    k, n = w.shape
    w = f64(np.asarray(w, np.float32).astype(ml_dtypes.bfloat16)).reshape(k // 32, 32, n)
    amax = np.abs(w).max(1)
    byte = np.clip(np.where(amax > 0, np.frexp(amax)[1] - 1 + 127 - 7, 1), 1, 254)
    scaled = (w * np.exp2(127.0 - byte)[:, None, :]).reshape(k, n).astype(np.float32)
    words = np.ascontiguousarray(scaled.reshape(k // 512, 128, 4, n).transpose(0, 1, 3, 2)).astype(ml_dtypes.float8_e4m3fn).view(np.uint8)
    return words, np.ascontiguousarray(byte.astype(np.uint8).reshape(k // 512, 16, n))


def unpack_weight(words, scales):
    g, p, n, _ = words.shape
    vals = np.ascontiguousarray(words).view(ml_dtypes.float8_e4m3fn).astype(np.float64) * np.repeat(np.exp2(scales.astype(np.float64) - 127.0), 8, axis=1)[..., None]
    return vals.transpose(0, 1, 3, 2).reshape(g * 512, n)


def relu(v):
    return np.maximum(v, 0.0)


K, T, S, D, V, H, N, U = 512, 2048, 512, 4, 512, 512, 128, 1024
P = 2 ** 7


def setup_inputs():
    n = np.random.standard_normal
    s = mx_kscale(K)[:, None]
    u = mx_kscale(H)
    packed_xT = pack_weight(n((K, T)) * s)
    packed_w2 = pack_weight(n((H, N)) / np.sqrt(H) / u[:, None])
    return {
        "x_words": packed_xT[0],
        "x_scales": packed_xT[1],
        "w1": (n((K, H)) / np.sqrt(K) / s * u).astype(np.float32),
        "w2_words": packed_w2[0],
        "w2_scales": packed_w2[1],
        "gate": np.tile(np.random.uniform(0.2, 0.6, (D, 1, V)), (1, P, 1)).astype(np.float32),
        "emb": (0.5 * n((H, U)) * u[:, None]).astype(np.float32),
        "offs": striped(np.random.permutation(T)[:S]),
        "cell": striped(np.random.permutation(U)[:S]),
        "pos1": striped(np.random.permutation(U)[:V]),
        "pos2": striped(np.random.permutation(U)[:V]),
        "pos3": striped(np.random.permutation(U)[:V]),
        "pos4": striped(np.random.permutation(U)[:V]),
    }


def reference(x_words, x_scales, w1, w2_words, w2_scales, gate, emb, offs, cell, pos1, pos2, pos3, pos4):
    xq = unpack_weight(x_words, x_scales)[:, unstriped(offs)]
    up = np.zeros((H, U))
    up[:, unstriped(cell)] = relu(mxq(f64(w1), 0, "e4m3").T @ xq)
    z = up + f64(emb)
    y = relu(unpack_weight(w2_words, w2_scales).T @ mxq(z, 0, "e4m3"))
    return y[:, unstriped(pos1)] * f64(gate)[0, :1] + y[:, unstriped(pos2)] * f64(gate)[1, :1] + y[:, unstriped(pos3)] * f64(gate)[2, :1] + y[:, unstriped(pos4)] * f64(gate)[3, :1]

@@ -1,0 +1,151 @@
+from contextlib import ExitStack
+
+import concourse.mybir as mybir
+
+K, T, S, D, V, H, N, U = 512, 2048, 512, 4, 512, 512, 128, 1024
+FLOPS = 2 * K * H * S + 2 * H * N * U
+
+F32 = mybir.dt.float32
+BF16 = mybir.dt.bfloat16
+I32 = mybir.dt.int32
+U32 = mybir.dt.uint32
+U16 = mybir.dt.uint16
+U8 = mybir.dt.uint8
+FP8X4 = mybir.dt.float8_e4m3fn_x4
+ADD = mybir.AluOpType.add
+MULT = mybir.AluOpType.mult
+RELU = mybir.ActivationFunctionType.Relu
+
+P = 128
+PACK = 4
+HALF = S // 2
+CHUNK = 256
+W1_SPLIT = 80
+
+
+def load_scale_rows(queue, plane, rows):
+    for q in range(4):
+        queue.dma_start(plane[32 * q : 32 * q + 4, :].bitcast(I32), rows[4 * q : 4 * q + 4, :].bitcast(I32))
+
+
+def tile_picked_devox_relu_p_kernel(
+    tc, x_words, x_scales, w1, w2_words, w2_scales, gate, emb, offs, cell, pos1, pos2, pos3, pos4, out
+):
+    nc = tc.nc
+    with ExitStack() as ctx:
+        keep = ctx.enter_context(tc.tile_pool(name="keep", bufs=1))
+        psum = ctx.enter_context(tc.psum_pool(name="psum", bufs=1))
+
+        offs_sb = keep.tile([P, S // 16], U16, name="offs_sb")
+        cell_sb = keep.tile([P, S // 16], U16, name="cell_sb")
+        pos_sb = [keep.tile([P, V // 16], U16, name=f"pos_sb{d}") for d in range(D)]
+        xs_all = keep.tile([P, T], U8, name="xs_all", align_bytes=64)
+        xw_all = keep.tile([P, T], U32, name="xw_all", align_bytes=64)
+        w1_raw = keep.tile([P, PACK, H], F32, name="w1_raw")
+        emb_sb = [keep.tile([P, U], F32, name=f"emb_sb{t}") for t in range(PACK)]
+        w2w = keep.tile([P, N], U32, name="w2w", align_bytes=64)
+        w2s = keep.tile([P, N], U8, name="w2s", align_bytes=64)
+        gate_sb = keep.tile([P, D, V], F32, name="gate_sb")
+        up = [keep.tile([P, U], F32, name=f"up{t}") for t in range(PACK)]
+
+        nc.gpsimd.memset(xs_all[:].bitcast(I32), 0)
+        nc.gpsimd.memset(w2s[:].bitcast(I32), 0)
+        for t in range(PACK):
+            (nc.vector if t < 2 else nc.gpsimd).memset(up[t][:], 0.0)
+
+        nc.sync.dma_start(offs_sb[:], offs)
+        nc.sync.dma_start(w1_raw[:], w1.rearrange("(p j) c -> p j c", j=PACK))
+        load_scale_rows(nc.sync, xs_all, x_scales[0])
+        nc.sync.dma_start(xw_all[:].bitcast(I32), x_words[0].rearrange("p n t -> p (n t)").bitcast(I32))
+        nc.sync.dma_start(cell_sb[:], cell)
+        emb_rows = emb.rearrange("(p t) r -> p t r", t=PACK)
+        for t in range(PACK):
+            nc.sync.dma_start(emb_sb[t][:], emb_rows[:, t, :])
+        nc.sync.dma_start(w2w[:].bitcast(I32), w2_words[0].rearrange("p n t -> p (n t)").bitcast(I32))
+        load_scale_rows(nc.sync, w2s, w2_scales[0])
+        for d, pos in enumerate((pos1, pos2, pos3, pos4)):
+            nc.sync.dma_start(pos_sb[d][:], pos)
+        nc.sync.dma_start(gate_sb[:], gate.rearrange("d p v -> p d v"))
+
+        xs = keep.tile([P, S], U8, name="xs", align_bytes=64)
+        nc.vector.tensor_copy(xs[:], xs_all[:].indirect(offs_sb[:]))
+
+        w1_bf = keep.tile([P, PACK * P * PACK], BF16, name="w1_bf", align_bytes=64)
+        dst = w1_bf[:].rearrange("p (t m j) -> p m t j", t=PACK, j=PACK)
+        src = w1_raw[:].rearrange("p j (m t) -> p m t j", t=PACK)
+        nc.vector.tensor_copy(dst[:, :W1_SPLIT], src[:, :W1_SPLIT])
+        nc.scalar.copy(dst[:, W1_SPLIT:], src[:, W1_SPLIT:])
+        w1q = keep.tile([P, H], U32, name="w1q", align_bytes=64)
+        w1s = keep.tile([P, H], U8, name="w1s", align_bytes=64)
+        nc.vector.quantize_mx(out=w1q[:].bitcast(FP8X4), scales=w1s[:], in_=w1_bf[:])
+
+        xw = [keep.tile([P, HALF], U32, name=f"xw{a}", align_bytes=64) for a in range(2)]
+        for a in range(2):
+            nc.vector.tensor_copy(xw[a][:], xw_all[:].indirect(offs_sb[:, a * HALF // 16 : (a + 1) * HALF // 16]))
+
+        h = [keep.tile([P, S], F32, name=f"h{t}") for t in range(PACK)]
+        for t in range(PACK):
+            cols = slice(t * P, (t + 1) * P)
+            pieces = 2 if t == 0 else 1
+            accs = [psum.tile([P, S // pieces], F32, name=f"acc{t}_{a}", tag=f"bank{2 * t + a}") for a in range(pieces)]
+            for a in range(2):
+                nc.tensor.matmul_mx(
+                    out=accs[a][:] if pieces == 2 else accs[0][:, a * HALF : (a + 1) * HALF],
+                    lhsT=w1q[:, cols].bitcast(FP8X4),
+                    lhsT_scale=w1s[:, cols],
+                    rhs=xw[a][:].bitcast(FP8X4),
+                    rhs_scale=xs[:, a * HALF : (a + 1) * HALF],
+                    start=True,
+                    stop=True,
+                )
+            for a in range(pieces):
+                nc.scalar.activation(h[t][:, a * S // pieces : (a + 1) * S // pieces], accs[a][:], RELU)
+
+        zb = [keep.tile([P, PACK, U // 2], BF16, name=f"zb{b}") for b in range(2)]
+        for t in range(PACK):
+            pieces = 2 if t == 0 else 1
+            for a in range(pieces):
+                lo, hi = a * S // pieces, (a + 1) * S // pieces
+                nc.vector.tensor_copy(up[t][:].indirect(cell_sb[:, lo // 16 : hi // 16]), h[t][:, lo:hi])
+            adder = nc.vector if t == PACK - 1 else nc.gpsimd
+            for b in range(2):
+                cols = slice(b * U // 2, (b + 1) * U // 2)
+                adder.tensor_tensor(zb[b][:, t, :], up[t][:, cols], emb_sb[t][:, cols], ADD)
+
+        y = keep.tile([P, U], F32, name="y")
+        n_chunks = U // CHUNK
+        z4 = [keep.tile([P, CHUNK * PACK], BF16, name=f"z4_{c}", align_bytes=64) for c in range(n_chunks)]
+        for c in range(n_chunks):
+            b, c0 = divmod(c * CHUNK, U // 2)
+            dst = z4[c][:].rearrange("p (r i t) -> p r t i", i=4, t=PACK)
+            src = zb[b][:, :, c0 : c0 + CHUNK].rearrange("p t (r i) -> p r t i", i=4)
+            if b == 0:
+                nc.scalar.copy(dst, src)
+            else:
+                nc.vector.tensor_copy(dst, src)
+        for c in (2, 0, 3, 1):
+            zq = keep.tile([P, CHUNK], U32, name=f"zq{c}", align_bytes=64)
+            zs = keep.tile([P, CHUNK], U8, name=f"zs{c}", align_bytes=64)
+            nc.vector.quantize_mx(out=zq[:].bitcast(FP8X4), scales=zs[:], in_=z4[c][:])
+            acc = psum.tile([P, CHUNK], F32, name=f"yacc{c}", tag=f"bank{c}")
+            nc.tensor.matmul_mx(
+                out=acc[:],
+                lhsT=w2w[:].bitcast(FP8X4),
+                lhsT_scale=w2s[:],
+                rhs=zq[:].bitcast(FP8X4),
+                rhs_scale=zs[:],
+                start=True,
+                stop=True,
+            )
+            nc.scalar.activation(y[:, c * CHUNK : (c + 1) * CHUNK], acc[:], RELU)
+
+        terms = keep.tile([P, D, V], F32, name="terms")
+        for d in range(D):
+            nc.vector.tensor_tensor(terms[:, d, :], y[:].indirect(pos_sb[d][:]), gate_sb[:, d, :], MULT)
+        pair = keep.tile([P, 2, V], F32, name="pair")
+        nc.vector.tensor_tensor(pair[:], terms[:, 0:2, :], terms[:, 2:4, :], ADD)
+        for a, queue in enumerate((nc.sync, nc.scalar)):
+            cols = slice(a * V // 2, (a + 1) * V // 2)
+            res = keep.tile([P, V // 2], F32, name=f"res{a}")
+            nc.vector.tensor_tensor(res[:], pair[:, 0, cols], pair[:, 1, cols], ADD)
+            queue.dma_start(out[:, cols], res[:])

@@ -1,6 +1,7 @@
 from contextlib import ExitStack
 
 import concourse.mybir as mybir
+from concourse.masks import make_identity
 
 K, T, S, D, V, H, N, U = 512, 2048, 512, 4, 512, 512, 128, 1024
 FLOPS = 2 * K * H * S + 2 * H * N * U
@@ -14,18 +15,25 @@ U8 = mybir.dt.uint8
 FP8X4 = mybir.dt.float8_e4m3fn_x4
 ADD = mybir.AluOpType.add
 MULT = mybir.AluOpType.mult
+COPY = mybir.ActivationFunctionType.Copy
 RELU = mybir.ActivationFunctionType.Relu
 
 P = 128
 PACK = 4
 HALF = S // 2
-CHUNK = 256
+FIRST = 128
+CHUNKS = ((0, 256), (256, 512), (512, 640), (640, 768), (768, 1024))
+SCALAR_CHUNKS = 4
 W1_SPLIT = 80
 
 
 def load_scale_rows(queue, plane, rows):
     for q in range(4):
         queue.dma_start(plane[32 * q : 32 * q + 4, :].bitcast(I32), rows[4 * q : 4 * q + 4, :].bitcast(I32))
+
+
+def blocks(ap):
+    return ap.rearrange("p (b r) -> p b r", r=P)
 
 
 def tile_picked_devox_relu_p_kernel(
@@ -45,7 +53,9 @@ def tile_picked_devox_relu_p_kernel(
         emb_sb = [keep.tile([P, U], F32, name=f"emb_sb{t}") for t in range(PACK)]
         w2w = keep.tile([P, N], U32, name="w2w", align_bytes=64)
         w2s = keep.tile([P, N], U8, name="w2s", align_bytes=64)
-        gate_sb = keep.tile([P, D, V], F32, name="gate_sb")
+        gate_rows = keep.tile([P, V], F32, name="gate_rows")
+        gate_last = keep.tile([P, V], F32, name="gate_last")
+        ident = keep.tile([P, P], F32, name="ident")
         up = [keep.tile([P, U], F32, name=f"up{t}") for t in range(PACK)]
 
         nc.gpsimd.memset(xs_all[:].bitcast(I32), 0)
@@ -58,6 +68,7 @@ def tile_picked_devox_relu_p_kernel(
         load_scale_rows(nc.sync, xs_all, x_scales[0])
         nc.sync.dma_start(xw_all[:].bitcast(I32), x_words[0].rearrange("p n t -> p (n t)").bitcast(I32))
         nc.sync.dma_start(cell_sb[:], cell)
+        nc.sync.dma_start(gate_rows[:], gate.rearrange("d (a b) v -> (d a) b v", b=D)[:, 0, :])
         emb_rows = emb.rearrange("(p t) r -> p t r", t=PACK)
         for t in range(PACK):
             nc.sync.dma_start(emb_sb[t][:], emb_rows[:, t, :])
@@ -65,7 +76,8 @@ def tile_picked_devox_relu_p_kernel(
         load_scale_rows(nc.sync, w2s, w2_scales[0])
         for d, pos in enumerate((pos1, pos2, pos3, pos4)):
             nc.sync.dma_start(pos_sb[d][:], pos)
-        nc.sync.dma_start(gate_sb[:], gate.rearrange("d p v -> p d v"))
+        nc.sync.dma_start(gate_last[:], gate[D - 1])
+        make_identity(nc, ident[:])
 
         xs = keep.tile([P, S], U8, name="xs", align_bytes=64)
         nc.vector.tensor_copy(xs[:], xs_all[:].indirect(offs_sb[:]))
@@ -84,50 +96,65 @@ def tile_picked_devox_relu_p_kernel(
             nc.vector.tensor_copy(xw[a][:], xw_all[:].indirect(offs_sb[:, a * HALF // 16 : (a + 1) * HALF // 16]))
 
         h = [keep.tile([P, S], F32, name=f"h{t}") for t in range(PACK)]
+        pieces = [[(0, FIRST), (FIRST, S)] if t == 0 else [(0, S)] for t in range(PACK)]
+        bank = 0
         for t in range(PACK):
             cols = slice(t * P, (t + 1) * P)
-            pieces = 2 if t == 0 else 1
-            accs = [psum.tile([P, S // pieces], F32, name=f"acc{t}_{a}", tag=f"bank{2 * t + a}") for a in range(pieces)]
-            for a in range(2):
-                nc.tensor.matmul_mx(
-                    out=accs[a][:] if pieces == 2 else accs[0][:, a * HALF : (a + 1) * HALF],
-                    lhsT=w1q[:, cols].bitcast(FP8X4),
-                    lhsT_scale=w1s[:, cols],
-                    rhs=xw[a][:].bitcast(FP8X4),
-                    rhs_scale=xs[:, a * HALF : (a + 1) * HALF],
-                    start=True,
-                    stop=True,
-                )
-            for a in range(pieces):
-                nc.scalar.activation(h[t][:, a * S // pieces : (a + 1) * S // pieces], accs[a][:], RELU)
+            for lo, hi in pieces[t]:
+                acc = psum.tile([P, hi - lo], F32, name=f"acc{t}_{lo}", tag=f"bank{bank}")
+                bank += 1
+                for a in range(2):
+                    a_lo, a_hi = max(lo, a * HALF), min(hi, (a + 1) * HALF)
+                    if a_lo < a_hi:
+                        nc.tensor.matmul_mx(
+                            out=acc[:, a_lo - lo : a_hi - lo],
+                            lhsT=w1q[:, cols].bitcast(FP8X4),
+                            lhsT_scale=w1s[:, cols],
+                            rhs=xw[a][:, a_lo - a * HALF : a_hi - a * HALF].bitcast(FP8X4),
+                            rhs_scale=xs[:, a_lo:a_hi],
+                            start=True,
+                            stop=True,
+                        )
+                nc.scalar.activation(h[t][:, lo:hi], acc[:], RELU)
 
-        zb = [keep.tile([P, PACK, U // 2], BF16, name=f"zb{b}") for b in range(2)]
+        n_blocks = V // P
+        gate_ps = psum.tile([P, n_blocks, P], F32, name="gate_ps", tag="bank7")
+        for c in range(n_blocks):
+            nc.tensor.transpose(gate_ps[:, c, :], gate_rows[:, c * P : (c + 1) * P], ident[:])
+        gate_col = keep.tile([P, n_blocks, D - 1], F32, name="gate_col")
+        nc.scalar.copy(gate_col[:], gate_ps[:].rearrange("p c (d a) -> p c d a", d=D)[:, :, : D - 1, 0])
+
+        early = keep.tile([P, 2, U], BF16, name="early")
+        late = keep.tile([P, U // P, 2, P], BF16, name="late")
         for t in range(PACK):
-            pieces = 2 if t == 0 else 1
-            for a in range(pieces):
-                lo, hi = a * S // pieces, (a + 1) * S // pieces
+            for lo, hi in pieces[t]:
                 nc.vector.tensor_copy(up[t][:].indirect(cell_sb[:, lo // 16 : hi // 16]), h[t][:, lo:hi])
-            adder = nc.vector if t == PACK - 1 else nc.gpsimd
-            for b in range(2):
-                cols = slice(b * U // 2, (b + 1) * U // 2)
-                adder.tensor_tensor(zb[b][:, t, :], up[t][:, cols], emb_sb[t][:, cols], ADD)
+            if t < 2:
+                nc.gpsimd.tensor_tensor(early[:, t, :], up[t][:], emb_sb[t][:], ADD)
+            elif t == 2:
+                nc.gpsimd.tensor_tensor(late[:, :, 0, :], blocks(up[t][:]), blocks(emb_sb[t][:]), ADD)
+        t = PACK - 1
+        for lo, hi in ((0, 256), (768, 1024), (256, 768)):
+            nc.vector.tensor_tensor(late[:, lo // P : hi // P, 1, :], blocks(up[t][:, lo:hi]), blocks(emb_sb[t][:, lo:hi]), ADD)
 
         y = keep.tile([P, U], F32, name="y")
-        n_chunks = U // CHUNK
-        z4 = [keep.tile([P, CHUNK * PACK], BF16, name=f"z4_{c}", align_bytes=64) for c in range(n_chunks)]
-        for c in range(n_chunks):
-            b, c0 = divmod(c * CHUNK, U // 2)
-            dst = z4[c][:].rearrange("p (r i t) -> p r t i", i=4, t=PACK)
-            src = zb[b][:, :, c0 : c0 + CHUNK].rearrange("p t (r i) -> p r t i", i=4)
-            if b == 0:
+        z4 = [keep.tile([P, (hi - lo) * PACK], BF16, name=f"z4_{lo}", align_bytes=64) for lo, hi in CHUNKS]
+        for c, (lo, hi) in enumerate(CHUNKS):
+            dst = z4[c][:].rearrange("p (r t) -> p r t", t=PACK)[:, :, 0:2]
+            nc.scalar.copy(dst, early[:, :, lo:hi].rearrange("p t r -> p r t"))
+        for c, (lo, hi) in enumerate(CHUNKS):
+            dst = z4[c][:].rearrange("p (b r t) -> p b r t", r=P, t=PACK)[:, :, :, 2:4]
+            src = late[:, lo // P : hi // P].rearrange("p b t r -> p b r t")
+            if c < SCALAR_CHUNKS:
                 nc.scalar.copy(dst, src)
             else:
                 nc.vector.tensor_copy(dst, src)
-        for c in (2, 0, 3, 1):
-            zq = keep.tile([P, CHUNK], U32, name=f"zq{c}", align_bytes=64)
-            zs = keep.tile([P, CHUNK], U8, name=f"zs{c}", align_bytes=64)
+        for c in (4, 0, 1, 2, 3):
+            lo, hi = CHUNKS[c]
+            zq = keep.tile([P, hi - lo], U32, name=f"zq{c}", align_bytes=64)
+            zs = keep.tile([P, hi - lo], U8, name=f"zs{c}", align_bytes=64)
             nc.vector.quantize_mx(out=zq[:].bitcast(FP8X4), scales=zs[:], in_=z4[c][:])
-            acc = psum.tile([P, CHUNK], F32, name=f"yacc{c}", tag=f"bank{c}")
+            acc = psum.tile([P, hi - lo], F32, name=f"yacc{c}", tag=f"bank{c}")
             nc.tensor.matmul_mx(
                 out=acc[:],
                 lhsT=w2w[:].bitcast(FP8X4),
@@ -137,15 +164,40 @@ def tile_picked_devox_relu_p_kernel(
                 start=True,
                 stop=True,
             )
-            nc.scalar.activation(y[:, c * CHUNK : (c + 1) * CHUNK], acc[:], RELU)
+            nc.scalar.activation(y[:, lo:hi], acc[:], RELU)
 
-        terms = keep.tile([P, D, V], F32, name="terms")
-        for d in range(D):
-            nc.vector.tensor_tensor(terms[:, d, :], y[:].indirect(pos_sb[d][:]), gate_sb[:, d, :], MULT)
-        pair = keep.tile([P, 2, V], F32, name="pair")
-        nc.vector.tensor_tensor(pair[:], terms[:, 0:2, :], terms[:, 2:4, :], ADD)
+        sums = [psum.tile([P, V // 2], F32, name=f"sum{a}", tag=f"bank{6 + a}") for a in range(2)]
+        turned = []
+
+        def fetch_and_turn(d):
+            picked = keep.tile([P, V], F32, name=f"picked{d}")
+            nc.vector.tensor_copy(picked[:], y[:].indirect(pos_sb[d][:]))
+            turned.append([psum.tile([P, 2, P], F32, name=f"turned{d}_{a}", tag=f"bank{2 * d + a}") for a in range(2)])
+            for c in range(n_blocks):
+                nc.tensor.transpose(turned[d][c // 2][:, c % 2, :], picked[:, c * P : (c + 1) * P], ident[:])
+
+        def weigh_and_sum(d):
+            for c in range(n_blocks):
+                scaled = keep.tile([P, P], F32, name=f"scaled{d}_{c}")
+                nc.scalar.activation(scaled[:], turned[d][c // 2][:, c % 2, :], COPY, scale=gate_col[:, c, d : d + 1])
+                nc.tensor.matmul(
+                    sums[c // 2][:, (c % 2) * P : (c % 2 + 1) * P],
+                    scaled[:],
+                    ident[:],
+                    start=(d == 0 and c % 2 == 0),
+                    stop=(d == D - 2 and c % 2 == 1),
+                    is_transpose=True,
+                )
+
+        fetch_and_turn(0)
+        for d in range(1, D - 1):
+            fetch_and_turn(d)
+            weigh_and_sum(d - 1)
+        weigh_and_sum(D - 2)
+        last = keep.tile([P, V], F32, name="last")
+        nc.vector.tensor_tensor(last[:], y[:].indirect(pos_sb[D - 1][:]), gate_last[:], MULT)
         for a, queue in enumerate((nc.sync, nc.scalar)):
             cols = slice(a * V // 2, (a + 1) * V // 2)
             res = keep.tile([P, V // 2], F32, name=f"res{a}")
-            nc.vector.tensor_tensor(res[:], pair[:, 0, cols], pair[:, 1, cols], ADD)
+            nc.vector.tensor_tensor(res[:], sums[a][:], last[:, cols], ADD)
             queue.dma_start(out[:, cols], res[:])

@@ -53,15 +53,15 @@ def tile_picked_devox_relu_p_kernel(
         emb_sb = [keep.tile([P, U], F32, name=f"emb_sb{t}") for t in range(PACK)]
         w2w = keep.tile([P, N], U32, name="w2w", align_bytes=64)
         w2s = keep.tile([P, N], U8, name="w2s", align_bytes=64)
-        gate_rows = keep.tile([P, V], F32, name="gate_rows")
+        gate_rows = keep.tile([P, V], F32, name="gate_rows", tag="gate_rows", align_bytes=64)
         gate_last = keep.tile([P, V], F32, name="gate_last")
         ident = keep.tile([P, P], F32, name="ident")
-        up = [keep.tile([P, U], F32, name=f"up{t}") for t in range(PACK)]
+        up = [keep.tile([P, U], F32, name=f"up{t}") for t in range(2)]
 
         nc.gpsimd.memset(xs_all[:].bitcast(I32), 0)
         nc.gpsimd.memset(w2s[:].bitcast(I32), 0)
-        for t in range(PACK):
-            (nc.vector if t < 2 else nc.gpsimd).memset(up[t][:], 0.0)
+        for t in range(2):
+            nc.vector.memset(up[t][:], 0.0)
 
         nc.sync.dma_start(offs_sb[:], offs)
         nc.sync.dma_start(w1_raw[:], w1.rearrange("(p j) c -> p j c", j=PACK))
@@ -82,7 +82,7 @@ def tile_picked_devox_relu_p_kernel(
         xs = keep.tile([P, S], U8, name="xs", align_bytes=64)
         nc.vector.tensor_copy(xs[:], xs_all[:].indirect(offs_sb[:]))
 
-        w1_bf = keep.tile([P, PACK * P * PACK], BF16, name="w1_bf", align_bytes=64)
+        w1_bf = keep.tile([P, PACK * P * PACK], BF16, name="w1_bf", tag="w1_bf", align_bytes=64)
         dst = w1_bf[:].rearrange("p (t m j) -> p m t j", t=PACK, j=PACK)
         src = w1_raw[:].rearrange("p j (m t) -> p m t j", t=PACK)
         nc.vector.tensor_copy(dst[:, :W1_SPLIT], src[:, :W1_SPLIT])
@@ -124,6 +124,9 @@ def tile_picked_devox_relu_p_kernel(
         gate_col = keep.tile([P, n_blocks, D - 1], F32, name="gate_col")
         nc.scalar.copy(gate_col[:], gate_ps[:].rearrange("p c (d a) -> p c d a", d=D)[:, :, : D - 1, 0])
 
+        for t, tag in ((2, "w1_bf"), (3, "gate_rows")):
+            up.append(keep.tile([P, U], F32, name=f"up{t}", tag=tag, align_bytes=64))
+            nc.gpsimd.memset(up[t][:], 0.0)
         early = keep.tile([P, 2, U], BF16, name="early")
         late = keep.tile([P, U // P, 2, P], BF16, name="late")
         for t in range(PACK):

@@ -20,19 +20,22 @@ RELU = mybir.ActivationFunctionType.Relu
 
 P = 128
 PACK = 4
+PER_COLUMN = 16
 HALF = S // 2
 FIRST = 128
 CHUNKS = ((0, 256), (256, 512), (512, 640), (640, 768), (768, 1024))
 SCALAR_CHUNKS = 4
+LAST_ADDS = ((0, 256), (768, 1024), (256, 768))
+QUANTISE_ORDER = (SCALAR_CHUNKS, *range(SCALAR_CHUNKS))
 W1_SPLIT = 80
 
 
-def load_scale_rows(queue, plane, rows):
+def load_scale_rows(queue, scale_tile, rows):
     for q in range(4):
-        queue.dma_start(plane[32 * q : 32 * q + 4, :].bitcast(I32), rows[4 * q : 4 * q + 4, :].bitcast(I32))
+        queue.dma_start(scale_tile[32 * q : 32 * q + 4, :].bitcast(I32), rows[4 * q : 4 * q + 4, :].bitcast(I32))
 
 
-def blocks(ap):
+def by_128(ap):
     return ap.rearrange("p (b r) -> p b r", r=P)
 
 
@@ -44,9 +47,9 @@ def tile_picked_devox_relu_p_kernel(
         keep = ctx.enter_context(tc.tile_pool(name="keep", bufs=1))
         psum = ctx.enter_context(tc.psum_pool(name="psum", bufs=1))
 
-        offs_sb = keep.tile([P, S // 16], U16, name="offs_sb")
-        cell_sb = keep.tile([P, S // 16], U16, name="cell_sb")
-        pos_sb = [keep.tile([P, V // 16], U16, name=f"pos_sb{d}") for d in range(D)]
+        offs_sb = keep.tile([P, S // PER_COLUMN], U16, name="offs_sb")
+        cell_sb = keep.tile([P, S // PER_COLUMN], U16, name="cell_sb")
+        pos_sb = [keep.tile([P, V // PER_COLUMN], U16, name=f"pos_sb{d}") for d in range(D)]
         xs_all = keep.tile([P, T], U8, name="xs_all", align_bytes=64)
         xw_all = keep.tile([P, T], U32, name="xw_all", align_bytes=64)
         w1_raw = keep.tile([P, PACK, H], F32, name="w1_raw")
@@ -83,39 +86,40 @@ def tile_picked_devox_relu_p_kernel(
         nc.vector.tensor_copy(xs[:], xs_all[:].indirect(offs_sb[:]))
 
         w1_bf = keep.tile([P, PACK * P * PACK], BF16, name="w1_bf", tag="w1_bf", align_bytes=64)
-        dst = w1_bf[:].rearrange("p (t m j) -> p m t j", t=PACK, j=PACK)
-        src = w1_raw[:].rearrange("p j (m t) -> p m t j", t=PACK)
-        nc.vector.tensor_copy(dst[:, :W1_SPLIT], src[:, :W1_SPLIT])
-        nc.scalar.copy(dst[:, W1_SPLIT:], src[:, W1_SPLIT:])
+        w1_to = w1_bf[:].rearrange("p (t m j) -> p m t j", t=PACK, j=PACK)
+        w1_from = w1_raw[:].rearrange("p j (m t) -> p m t j", t=PACK)
+        nc.vector.tensor_copy(w1_to[:, :W1_SPLIT], w1_from[:, :W1_SPLIT])
+        nc.scalar.copy(w1_to[:, W1_SPLIT:], w1_from[:, W1_SPLIT:])
         w1q = keep.tile([P, H], U32, name="w1q", align_bytes=64)
         w1s = keep.tile([P, H], U8, name="w1s", align_bytes=64)
         nc.vector.quantize_mx(out=w1q[:].bitcast(FP8X4), scales=w1s[:], in_=w1_bf[:])
 
         xw = [keep.tile([P, HALF], U32, name=f"xw{a}", align_bytes=64) for a in range(2)]
         for a in range(2):
-            nc.vector.tensor_copy(xw[a][:], xw_all[:].indirect(offs_sb[:, a * HALF // 16 : (a + 1) * HALF // 16]))
+            entries = offs_sb[:, a * HALF // PER_COLUMN : (a + 1) * HALF // PER_COLUMN]
+            nc.vector.tensor_copy(xw[a][:], xw_all[:].indirect(entries))
 
         h = [keep.tile([P, S], F32, name=f"h{t}") for t in range(PACK)]
         pieces = [[(0, FIRST), (FIRST, S)] if t == 0 else [(0, S)] for t in range(PACK)]
         bank = 0
         for t in range(PACK):
-            cols = slice(t * P, (t + 1) * P)
+            plane_cols = slice(t * P, (t + 1) * P)
             for lo, hi in pieces[t]:
-                acc = psum.tile([P, hi - lo], F32, name=f"acc{t}_{lo}", tag=f"bank{bank}")
+                h_acc = psum.tile([P, hi - lo], F32, name=f"acc{t}_{lo}", tag=f"bank{bank}")
                 bank += 1
                 for a in range(2):
                     a_lo, a_hi = max(lo, a * HALF), min(hi, (a + 1) * HALF)
                     if a_lo < a_hi:
                         nc.tensor.matmul_mx(
-                            out=acc[:, a_lo - lo : a_hi - lo],
-                            lhsT=w1q[:, cols].bitcast(FP8X4),
-                            lhsT_scale=w1s[:, cols],
+                            out=h_acc[:, a_lo - lo : a_hi - lo],
+                            lhsT=w1q[:, plane_cols].bitcast(FP8X4),
+                            lhsT_scale=w1s[:, plane_cols],
                             rhs=xw[a][:, a_lo - a * HALF : a_hi - a * HALF].bitcast(FP8X4),
                             rhs_scale=xs[:, a_lo:a_hi],
                             start=True,
                             stop=True,
                         )
-                nc.scalar.activation(h[t][:, lo:hi], acc[:], RELU)
+                nc.scalar.activation(h[t][:, lo:hi], h_acc[:], RELU)
 
         n_blocks = V // P
         gate_ps = psum.tile([P, n_blocks, P], F32, name="gate_ps", tag="bank7")
@@ -124,42 +128,43 @@ def tile_picked_devox_relu_p_kernel(
         gate_col = keep.tile([P, n_blocks, D - 1], F32, name="gate_col")
         nc.scalar.copy(gate_col[:], gate_ps[:].rearrange("p c (d a) -> p c d a", d=D)[:, :, : D - 1, 0])
 
-        for t, tag in ((2, "w1_bf"), (3, "gate_rows")):
-            up.append(keep.tile([P, U], F32, name=f"up{t}", tag=tag, align_bytes=64))
+        for t, used_up in ((2, "w1_bf"), (3, "gate_rows")):
+            up.append(keep.tile([P, U], F32, name=f"up{t}", tag=used_up, align_bytes=64))
             nc.gpsimd.memset(up[t][:], 0.0)
-        early = keep.tile([P, 2, U], BF16, name="early")
-        late = keep.tile([P, U // P, 2, P], BF16, name="late")
+
+        early = keep.tile([P, 2, U], F32, name="early")
+        late = keep.tile([P, U // P, 2, P], F32, name="late")
         for t in range(PACK):
             for lo, hi in pieces[t]:
-                nc.vector.tensor_copy(up[t][:].indirect(cell_sb[:, lo // 16 : hi // 16]), h[t][:, lo:hi])
+                nc.vector.tensor_copy(up[t][:].indirect(cell_sb[:, lo // PER_COLUMN : hi // PER_COLUMN]), h[t][:, lo:hi])
             if t < 2:
                 nc.gpsimd.tensor_tensor(early[:, t, :], up[t][:], emb_sb[t][:], ADD)
             elif t == 2:
-                nc.gpsimd.tensor_tensor(late[:, :, 0, :], blocks(up[t][:]), blocks(emb_sb[t][:]), ADD)
-        t = PACK - 1
-        for lo, hi in ((0, 256), (768, 1024), (256, 768)):
-            nc.vector.tensor_tensor(late[:, lo // P : hi // P, 1, :], blocks(up[t][:, lo:hi]), blocks(emb_sb[t][:, lo:hi]), ADD)
+                nc.gpsimd.tensor_tensor(late[:, :, 0, :], by_128(up[t][:]), by_128(emb_sb[t][:]), ADD)
+        for lo, hi in LAST_ADDS:
+            nc.vector.tensor_tensor(late[:, lo // P : hi // P, 1, :], by_128(up[3][:, lo:hi]), by_128(emb_sb[3][:, lo:hi]), ADD)
 
         y = keep.tile([P, U], F32, name="y")
         z4 = [keep.tile([P, (hi - lo) * PACK], BF16, name=f"z4_{lo}", align_bytes=64) for lo, hi in CHUNKS]
         for c, (lo, hi) in enumerate(CHUNKS):
-            dst = z4[c][:].rearrange("p (r t) -> p r t", t=PACK)[:, :, 0:2]
-            nc.scalar.copy(dst, early[:, :, lo:hi].rearrange("p t r -> p r t"))
+            early_to = z4[c][:].rearrange("p (r t) -> p r t", t=PACK)[:, :, 0:2]
+            nc.scalar.copy(early_to, early[:, :, lo:hi].rearrange("p t r -> p r t"))
         for c, (lo, hi) in enumerate(CHUNKS):
-            dst = z4[c][:].rearrange("p (b r t) -> p b r t", r=P, t=PACK)[:, :, :, 2:4]
-            src = late[:, lo // P : hi // P].rearrange("p b t r -> p b r t")
+            late_to = z4[c][:].rearrange("p (b r t) -> p b r t", r=P, t=PACK)[:, :, :, 2:4]
+            late_from = late[:, lo // P : hi // P].rearrange("p b t r -> p b r t")
             if c < SCALAR_CHUNKS:
-                nc.scalar.copy(dst, src)
+                nc.scalar.copy(late_to, late_from)
             else:
-                nc.vector.tensor_copy(dst, src)
-        for c in (4, 0, 1, 2, 3):
+                nc.vector.tensor_copy(late_to, late_from)
+
+        for c in QUANTISE_ORDER:
             lo, hi = CHUNKS[c]
             zq = keep.tile([P, hi - lo], U32, name=f"zq{c}", align_bytes=64)
             zs = keep.tile([P, hi - lo], U8, name=f"zs{c}", align_bytes=64)
             nc.vector.quantize_mx(out=zq[:].bitcast(FP8X4), scales=zs[:], in_=z4[c][:])
-            acc = psum.tile([P, hi - lo], F32, name=f"yacc{c}", tag=f"bank{c}")
+            y_acc = psum.tile([P, hi - lo], F32, name=f"yacc{c}", tag=f"bank{c}")
             nc.tensor.matmul_mx(
-                out=acc[:],
+                out=y_acc[:],
                 lhsT=w2w[:].bitcast(FP8X4),
                 lhsT_scale=w2s[:],
                 rhs=zq[:].bitcast(FP8X4),
@@ -167,7 +172,7 @@ def tile_picked_devox_relu_p_kernel(
                 start=True,
                 stop=True,
             )
-            nc.scalar.activation(y[:, lo:hi], acc[:], RELU)
+            nc.scalar.activation(y[:, lo:hi], y_acc[:], RELU)
 
         sums = [psum.tile([P, V // 2], F32, name=f"sum{a}", tag=f"bank{6 + a}") for a in range(2)]
         turned = []
@@ -197,10 +202,11 @@ def tile_picked_devox_relu_p_kernel(
             fetch_and_turn(d)
             weigh_and_sum(d - 1)
         weigh_and_sum(D - 2)
+
         last = keep.tile([P, V], F32, name="last")
         nc.vector.tensor_tensor(last[:], y[:].indirect(pos_sb[D - 1][:]), gate_last[:], MULT)
         for a, queue in enumerate((nc.sync, nc.scalar)):
-            cols = slice(a * V // 2, (a + 1) * V // 2)
+            out_cols = slice(a * V // 2, (a + 1) * V // 2)
             res = keep.tile([P, V // 2], F32, name=f"res{a}")
-            nc.vector.tensor_tensor(res[:], sums[a][:], last[:, cols], ADD)
-            queue.dma_start(out[:, cols], res[:])
+            nc.vector.tensor_tensor(res[:], sums[a][:], last[:, out_cols], ADD)
+            queue.dma_start(out[:, out_cols], res[:])

@@ -23,10 +23,11 @@ PACK = 4
 PER_COLUMN = 16
 HALF = S // 2
 FIRST = 128
-CHUNKS = ((0, 256), (256, 512), (512, 640), (640, 768), (768, 1024))
-SCALAR_CHUNKS = 4
-LAST_ADDS = ((0, 256), (768, 1024), (256, 768))
-QUANTISE_ORDER = (SCALAR_CHUNKS, *range(SCALAR_CHUNKS))
+CHUNKS = ((0, 256), (256, 512), (512, 640), (768, 1024), (640, 768))
+SCALAR_CHUNKS = 3
+LAST_ADDS = ((0, 256), (640, 1024), (256, 640))
+QUANTISE_ORDER = (3, 4, 0, 1, 2)
+OWN = 640
 W1_SPLIT = 80
 
 
@@ -157,14 +158,19 @@ def tile_picked_devox_relu_p_kernel(
             else:
                 nc.vector.tensor_copy(late_to, late_from)
 
+        own_acc = psum.tile([P, U - OWN], F32, name="own_acc", tag="bank3")
         for c in QUANTISE_ORDER:
             lo, hi = CHUNKS[c]
             zq = keep.tile([P, hi - lo], U32, name=f"zq{c}", align_bytes=64)
             zs = keep.tile([P, hi - lo], U8, name=f"zs{c}", align_bytes=64)
             nc.vector.quantize_mx(out=zq[:].bitcast(FP8X4), scales=zs[:], in_=z4[c][:])
-            y_acc = psum.tile([P, hi - lo], F32, name=f"yacc{c}", tag=f"bank{c}")
+            if c < SCALAR_CHUNKS:
+                y_acc = psum.tile([P, hi - lo], F32, name=f"yacc{c}", tag=f"bank{c}")
+                y_to = y_acc[:]
+            else:
+                y_to = own_acc[:, lo - OWN : hi - OWN]
             nc.tensor.matmul_mx(
-                out=y_acc[:],
+                out=y_to,
                 lhsT=w2w[:].bitcast(FP8X4),
                 lhsT_scale=w2s[:],
                 rhs=zq[:].bitcast(FP8X4),
@@ -172,14 +178,20 @@ def tile_picked_devox_relu_p_kernel(
                 start=True,
                 stop=True,
             )
-            nc.scalar.activation(y[:, lo:hi], y_acc[:], RELU)
+            if c == 4:
+                nc.scalar.activation(y[:, OWN:], own_acc[:], RELU)
+            elif c == 1:
+                nc.vector.tensor_scalar_max(y[:, lo:hi], y_acc[:], 0.0)
+            elif c != 3:
+                nc.scalar.activation(y[:, lo:hi], y_acc[:], RELU)
 
         sums = [psum.tile([P, V // 2], F32, name=f"sum{a}", tag=f"bank{6 + a}") for a in range(2)]
         turned = []
 
         def fetch_and_turn(d):
             picked = keep.tile([P, V], F32, name=f"picked{d}")
-            nc.vector.tensor_copy(picked[:], y[:].indirect(pos_sb[d][:]))
+            for a in range(2):
+                nc.vector.tensor_copy(picked[:, 256 * a : 256 * a + 256], y[:].indirect(pos_sb[d][:, 16 * a : 16 * a + 16]))
             turned.append([psum.tile([P, 2, P], F32, name=f"turned{d}_{a}", tag=f"bank{2 * d + a}") for a in range(2)])
             for c in range(n_blocks):
                 nc.tensor.transpose(turned[d][c // 2][:, c % 2, :], picked[:, c * P : (c + 1) * P], ident[:])
@@ -204,7 +216,8 @@ def tile_picked_devox_relu_p_kernel(
         weigh_and_sum(D - 2)
 
         last = keep.tile([P, V], F32, name="last")
-        nc.vector.tensor_tensor(last[:], y[:].indirect(pos_sb[D - 1][:]), gate_last[:], MULT)
+        for a in range(2):
+            nc.vector.tensor_tensor(last[:, 256 * a : 256 * a + 256], y[:].indirect(pos_sb[D - 1][:, 16 * a : 16 * a + 16]), gate_last[:, 256 * a : 256 * a + 256], MULT)
         for a, queue in enumerate((nc.sync, nc.scalar)):
             out_cols = slice(a * V // 2, (a + 1) * V // 2)
             res = keep.tile([P, V // 2], F32, name=f"res{a}")

@@ -180,8 +180,6 @@ def tile_picked_devox_relu_p_kernel(
             )
             if c == 4:
                 nc.scalar.activation(y[:, OWN:], own_acc[:], RELU)
-            elif c == 1:
-                nc.vector.tensor_scalar_max(y[:, lo:hi], y_acc[:], 0.0)
             elif c != 3:
                 nc.scalar.activation(y[:, lo:hi], y_acc[:], RELU)
 

@@ -22,7 +22,7 @@ P = 128
 PACK = 4
 PER_COLUMN = 16
 HALF = S // 2
-FIRST = 128
+PIECES = ((0, 0, 128), (1, 0, HALF), (0, 128, S), (1, HALF, S), (2, 0, S), (3, 0, S))
 CHUNKS = ((0, 256), (256, 512), (512, 640), (768, 1024), (640, 768))
 SCALAR_CHUNKS = 3
 LAST_ADDS = ((0, 256), (640, 1024), (256, 640))
@@ -101,26 +101,22 @@ def tile_picked_devox_relu_p_kernel(
             nc.vector.tensor_copy(xw[a][:], xw_all[:].indirect(entries))
 
         h = [keep.tile([P, S], F32, name=f"h{t}") for t in range(PACK)]
-        pieces = [[(0, FIRST), (FIRST, S)] if t == 0 else [(0, S)] for t in range(PACK)]
-        bank = 0
-        for t in range(PACK):
+        for bank, (t, lo, hi) in enumerate(PIECES):
             plane_cols = slice(t * P, (t + 1) * P)
-            for lo, hi in pieces[t]:
-                h_acc = psum.tile([P, hi - lo], F32, name=f"acc{t}_{lo}", tag=f"bank{bank}")
-                bank += 1
-                for a in range(2):
-                    a_lo, a_hi = max(lo, a * HALF), min(hi, (a + 1) * HALF)
-                    if a_lo < a_hi:
-                        nc.tensor.matmul_mx(
-                            out=h_acc[:, a_lo - lo : a_hi - lo],
-                            lhsT=w1q[:, plane_cols].bitcast(FP8X4),
-                            lhsT_scale=w1s[:, plane_cols],
-                            rhs=xw[a][:, a_lo - a * HALF : a_hi - a * HALF].bitcast(FP8X4),
-                            rhs_scale=xs[:, a_lo:a_hi],
-                            start=True,
-                            stop=True,
-                        )
-                nc.scalar.activation(h[t][:, lo:hi], h_acc[:], RELU)
+            h_acc = psum.tile([P, hi - lo], F32, name=f"acc{t}_{lo}", tag=f"bank{bank}")
+            for a in range(2):
+                a_lo, a_hi = max(lo, a * HALF), min(hi, (a + 1) * HALF)
+                if a_lo < a_hi:
+                    nc.tensor.matmul_mx(
+                        out=h_acc[:, a_lo - lo : a_hi - lo],
+                        lhsT=w1q[:, plane_cols].bitcast(FP8X4),
+                        lhsT_scale=w1s[:, plane_cols],
+                        rhs=xw[a][:, a_lo - a * HALF : a_hi - a * HALF].bitcast(FP8X4),
+                        rhs_scale=xs[:, a_lo:a_hi],
+                        start=True,
+                        stop=True,
+                    )
+            nc.scalar.activation(h[t][:, lo:hi], h_acc[:], RELU)
 
         n_blocks = V // P
         gate_ps = psum.tile([P, n_blocks, P], F32, name="gate_ps", tag="bank7")
@@ -135,9 +131,10 @@ def tile_picked_devox_relu_p_kernel(
 
         early = keep.tile([P, 2, U], F32, name="early")
         late = keep.tile([P, U // P, 2, P], F32, name="late")
-        for t in range(PACK):
-            for lo, hi in pieces[t]:
-                nc.vector.tensor_copy(up[t][:].indirect(cell_sb[:, lo // PER_COLUMN : hi // PER_COLUMN]), h[t][:, lo:hi])
+        for t, lo, hi in PIECES:
+            nc.vector.tensor_copy(up[t][:].indirect(cell_sb[:, lo // PER_COLUMN : hi // PER_COLUMN]), h[t][:, lo:hi])
+            if hi < S:
+                continue
             if t < 2:
                 nc.gpsimd.tensor_tensor(early[:, t, :], up[t][:], emb_sb[t][:], ADD)
             elif t == 2:

@@ -32,8 +32,8 @@ W1_SPLIT = 80
 
 
 def load_scale_rows(queue, scale_tile, rows):
-    for q in range(4):
-        queue.dma_start(scale_tile[32 * q : 32 * q + 4, :].bitcast(I32), rows[4 * q : 4 * q + 4, :].bitcast(I32))
+    for r in range(4):
+        queue.dma_start(scale_tile[r:P:32, :].bitcast(I32), rows[r:16:4, :].bitcast(I32))
 
 
 def by_128(ap):

@@ -15,7 +15,6 @@ U8 = mybir.dt.uint8
 FP8X4 = mybir.dt.float8_e4m3fn_x4
 ADD = mybir.AluOpType.add
 MULT = mybir.AluOpType.mult
-COPY = mybir.ActivationFunctionType.Copy
 RELU = mybir.ActivationFunctionType.Relu
 
 P = 128
@@ -28,12 +27,14 @@ SCALAR_CHUNKS = 3
 LAST_ADDS = ((0, 256), (640, 1024), (256, 640))
 QUANTISE_ORDER = (3, 4, 0, 1, 2)
 OWN = 640
+FETCH_WIDTHS = (512, 512, 128, 256)
+OUT_PARTS = ((0, 256), (256, 384), (384, 512))
 W1_SPLIT = 80
 
 
 def load_scale_rows(queue, scale_tile, rows):
-    for r in range(4):
-        queue.dma_start(scale_tile[r:P:32, :].bitcast(I32), rows[r:16:4, :].bitcast(I32))
+    for q in range(4):
+        queue.dma_start(scale_tile[32 * q : 32 * q + 4, :].bitcast(I32), rows[4 * q : 4 * q + 4, :].bitcast(I32))
 
 
 def by_128(ap):
@@ -53,12 +54,11 @@ def tile_picked_devox_relu_p_kernel(
         pos_sb = [keep.tile([P, V // PER_COLUMN], U16, name=f"pos_sb{d}") for d in range(D)]
         xs_all = keep.tile([P, T], U8, name="xs_all", align_bytes=64)
         xw_all = keep.tile([P, T], U32, name="xw_all", align_bytes=64)
-        w1_raw = keep.tile([P, PACK, H], F32, name="w1_raw")
+        w1_raw = keep.tile([P, PACK, H], F32, name="w1_raw", tag="w1_raw", align_bytes=64)
         emb_sb = [keep.tile([P, U], F32, name=f"emb_sb{t}") for t in range(PACK)]
         w2w = keep.tile([P, N], U32, name="w2w", align_bytes=64)
         w2s = keep.tile([P, N], U8, name="w2s", align_bytes=64)
-        gate_rows = keep.tile([P, V], F32, name="gate_rows", tag="gate_rows", align_bytes=64)
-        gate_last = keep.tile([P, V], F32, name="gate_last")
+        gate_sb = keep.tile([P, D, V], F32, name="gate_sb")
         ident = keep.tile([P, P], F32, name="ident")
         up = [keep.tile([P, U], F32, name=f"up{t}") for t in range(2)]
 
@@ -72,7 +72,6 @@ def tile_picked_devox_relu_p_kernel(
         load_scale_rows(nc.sync, xs_all, x_scales[0])
         nc.sync.dma_start(xw_all[:].bitcast(I32), x_words[0].rearrange("p n t -> p (n t)").bitcast(I32))
         nc.sync.dma_start(cell_sb[:], cell)
-        nc.sync.dma_start(gate_rows[:], gate.rearrange("d (a b) v -> (d a) b v", b=D)[:, 0, :])
         emb_rows = emb.rearrange("(p t) r -> p t r", t=PACK)
         for t in range(PACK):
             nc.sync.dma_start(emb_sb[t][:], emb_rows[:, t, :])
@@ -80,7 +79,7 @@ def tile_picked_devox_relu_p_kernel(
         load_scale_rows(nc.sync, w2s, w2_scales[0])
         for d, pos in enumerate((pos1, pos2, pos3, pos4)):
             nc.sync.dma_start(pos_sb[d][:], pos)
-        nc.sync.dma_start(gate_last[:], gate[D - 1])
+        nc.sync.dma_start(gate_sb[:], gate.rearrange("d p v -> p d v"))
         make_identity(nc, ident[:])
 
         xs = keep.tile([P, S], U8, name="xs", align_bytes=64)
@@ -118,14 +117,7 @@ def tile_picked_devox_relu_p_kernel(
                     )
             nc.scalar.activation(h[t][:, lo:hi], h_acc[:], RELU)
 
-        n_blocks = V // P
-        gate_ps = psum.tile([P, n_blocks, P], F32, name="gate_ps", tag="bank7")
-        for c in range(n_blocks):
-            nc.tensor.transpose(gate_ps[:, c, :], gate_rows[:, c * P : (c + 1) * P], ident[:])
-        gate_col = keep.tile([P, n_blocks, D - 1], F32, name="gate_col")
-        nc.scalar.copy(gate_col[:], gate_ps[:].rearrange("p c (d a) -> p c d a", d=D)[:, :, : D - 1, 0])
-
-        for t, used_up in ((2, "w1_bf"), (3, "gate_rows")):
+        for t, used_up in ((2, "w1_bf"), (3, "w1_raw")):
             up.append(keep.tile([P, U], F32, name=f"up{t}", tag=used_up, align_bytes=64))
             nc.gpsimd.memset(up[t][:], 0.0)
 
@@ -180,41 +172,28 @@ def tile_picked_devox_relu_p_kernel(
             elif c != 3:
                 nc.scalar.activation(y[:, lo:hi], y_acc[:], RELU)
 
-        sums = [psum.tile([P, V // 2], F32, name=f"sum{a}", tag=f"bank{6 + a}") for a in range(2)]
-        turned = []
-
-        def fetch_and_turn(d):
-            picked = keep.tile([P, V], F32, name=f"picked{d}")
-            for a in range(2):
-                nc.vector.tensor_copy(picked[:, 256 * a : 256 * a + 256], y[:].indirect(pos_sb[d][:, 16 * a : 16 * a + 16]))
-            turned.append([psum.tile([P, 2, P], F32, name=f"turned{d}_{a}", tag=f"bank{2 * d + a}") for a in range(2)])
-            for c in range(n_blocks):
-                nc.tensor.transpose(turned[d][c // 2][:, c % 2, :], picked[:, c * P : (c + 1) * P], ident[:])
-
-        def weigh_and_sum(d):
-            for c in range(n_blocks):
-                scaled = keep.tile([P, P], F32, name=f"scaled{d}_{c}")
-                nc.scalar.activation(scaled[:], turned[d][c // 2][:, c % 2, :], COPY, scale=gate_col[:, c, d : d + 1])
-                nc.tensor.matmul(
-                    sums[c // 2][:, (c % 2) * P : (c % 2 + 1) * P],
-                    scaled[:],
-                    ident[:],
-                    start=(d == 0 and c % 2 == 0),
-                    stop=(d == D - 2 and c % 2 == 1),
-                    is_transpose=True,
-                )
-
-        fetch_and_turn(0)
-        for d in range(1, D - 1):
-            fetch_and_turn(d)
-            weigh_and_sum(d - 1)
-        weigh_and_sum(D - 2)
-
-        last = keep.tile([P, V], F32, name="last")
-        for a in range(2):
-            nc.vector.tensor_tensor(last[:, 256 * a : 256 * a + 256], y[:].indirect(pos_sb[D - 1][:, 16 * a : 16 * a + 16]), gate_last[:, 256 * a : 256 * a + 256], MULT)
-        for a, queue in enumerate((nc.sync, nc.scalar)):
-            out_cols = slice(a * V // 2, (a + 1) * V // 2)
-            res = keep.tile([P, V // 2], F32, name=f"res{a}")
-            nc.vector.tensor_tensor(res[:], sums[a][:], last[:, out_cols], ADD)
-            queue.dma_start(out[:, out_cols], res[:])
+        terms = [keep.tile([P, V], F32, name=f"term{d}") for d in range(D)]
+        turned = [psum.tile([P, P], F32, name=f"turned{c}", tag=f"bank{c}") for c in range(V // P)]
+        sums = [psum.tile([P, hi - lo], F32, name=f"sum{lo}", tag=f"bank{5 + i}") for i, (lo, hi) in enumerate(OUT_PARTS)]
+        for d, width in enumerate(FETCH_WIDTHS):
+            for lo in range(0, V, width):
+                cols = slice(lo, lo + width)
+                entries = pos_sb[d][:, lo // PER_COLUMN : (lo + width) // PER_COLUMN]
+                nc.vector.tensor_tensor(terms[d][:, cols], y[:].indirect(entries), gate_sb[:, d, cols], MULT)
+                if d == D - 1:
+                    continue
+                for c in range(lo // P, (lo + width) // P):
+                    block = slice(c * P, (c + 1) * P)
+                    nc.tensor.matmul(
+                        turned[c][:], terms[d][:, block], ident[:], start=(d == 0), stop=(d == D - 2), is_transpose=True
+                    )
+                    if d == D - 2:
+                        summed = keep.tile([P, P], F32, name=f"summed{c}")
+                        nc.scalar.copy(summed[:], turned[c][:])
+                        part = max(0, c - 1)
+                        at = c * P - OUT_PARTS[part][0]
+                        nc.tensor.transpose(sums[part][:, at : at + P], summed[:], ident[:])
+        for (lo, hi), part_sum, queue in zip(OUT_PARTS, sums, (nc.sync, nc.scalar, nc.sync)):
+            res = keep.tile([P, hi - lo], F32, name=f"res{lo}")
+            nc.vector.tensor_tensor(res[:], part_sum[:], terms[D - 1][:, lo:hi], ADD)
+            queue.dma_start(out[:, lo:hi], res[:])

@@ -52,49 +52,42 @@ def tile_picked_devox_relu_p_kernel(
         offs_sb = keep.tile([P, S // PER_COLUMN], U16, name="offs_sb")
         cell_sb = keep.tile([P, S // PER_COLUMN], U16, name="cell_sb")
         pos_sb = [keep.tile([P, V // PER_COLUMN], U16, name=f"pos_sb{d}") for d in range(D)]
-        xs_all = keep.tile([P, T], U8, name="xs_all", align_bytes=64)
-        xw_all = keep.tile([P, T], U32, name="xw_all", align_bytes=64)
+        xs_all = keep.tile([P, T], U8, name="xs_all", tag="w1_bf", align_bytes=64)
+        xw_all = keep.tile([P, T], U32, name="xw_all", tag="xw_all", align_bytes=64)
         w1_raw = keep.tile([P, PACK, H], F32, name="w1_raw", tag="w1_raw", align_bytes=64)
-        emb_sb = [keep.tile([P, U], F32, name=f"emb_sb{t}") for t in range(PACK)]
-        w2w = keep.tile([P, N], U32, name="w2w", align_bytes=64)
-        w2s = keep.tile([P, N], U8, name="w2s", align_bytes=64)
-        gate_sb = keep.tile([P, D, V], F32, name="gate_sb")
         ident = keep.tile([P, P], F32, name="ident")
         up = [keep.tile([P, U], F32, name=f"up{t}") for t in range(2)]
 
         nc.gpsimd.memset(xs_all[:].bitcast(I32), 0)
-        nc.gpsimd.memset(w2s[:].bitcast(I32), 0)
-        for t in range(2):
-            nc.vector.memset(up[t][:], 0.0)
+        nc.vector.memset(up[0][:], 0.0)
+        nc.scalar.copy(up[1][:], up[0][:])
 
         nc.sync.dma_start(offs_sb[:], offs)
-        nc.sync.dma_start(w1_raw[:], w1.rearrange("(p j) c -> p j c", j=PACK))
-        load_scale_rows(nc.sync, xs_all, x_scales[0])
-        nc.sync.dma_start(xw_all[:].bitcast(I32), x_words[0].rearrange("p n t -> p (n t)").bitcast(I32))
         nc.sync.dma_start(cell_sb[:], cell)
-        emb_rows = emb.rearrange("(p t) r -> p t r", t=PACK)
-        for t in range(PACK):
-            nc.sync.dma_start(emb_sb[t][:], emb_rows[:, t, :])
-        nc.sync.dma_start(w2w[:].bitcast(I32), w2_words[0].rearrange("p n t -> p (n t)").bitcast(I32))
-        load_scale_rows(nc.sync, w2s, w2_scales[0])
+        nc.sync.dma_start(xs_all[0:P:8, :].bitcast(I32), x_scales[0].bitcast(I32))
+        nc.sync.dma_start(w1_raw[:], w1.rearrange("(p j) c -> p j c", j=PACK))
+        nc.sync.dma_start(xw_all[:].bitcast(I32), x_words[0].rearrange("p n t -> p (n t)").bitcast(I32))
         for d, pos in enumerate((pos1, pos2, pos3, pos4)):
             nc.sync.dma_start(pos_sb[d][:], pos)
-        nc.sync.dma_start(gate_sb[:], gate.rearrange("d p v -> p d v"))
         make_identity(nc, ident[:])
 
-        xs = keep.tile([P, S], U8, name="xs", align_bytes=64)
-        nc.vector.tensor_copy(xs[:], xs_all[:].indirect(offs_sb[:]))
+        xs_spread = keep.tile([P, S], U8, name="xs_spread", tag="xs_spread", align_bytes=64)
+        nc.vector.tensor_copy(xs_spread[:], xs_all[:].indirect(offs_sb[:]))
+        xs = keep.tile([P, S], U8, name="xs", tag="xs", align_bytes=64)
+        nc.vector.tensor_copy(xs[:].bitcast(I32), xs_spread[:].bitcast(I32))
+        for r in range(1, 4):
+            nc.scalar.dma_start(xs[r:P:32, :].bitcast(I32), xs_spread[8 * r : P : 32, :].bitcast(I32))
 
         w1_bf = keep.tile([P, PACK * P * PACK], BF16, name="w1_bf", tag="w1_bf", align_bytes=64)
         w1_to = w1_bf[:].rearrange("p (t m j) -> p m t j", t=PACK, j=PACK)
         w1_from = w1_raw[:].rearrange("p j (m t) -> p m t j", t=PACK)
         nc.vector.tensor_copy(w1_to[:, :W1_SPLIT], w1_from[:, :W1_SPLIT])
         nc.scalar.copy(w1_to[:, W1_SPLIT:], w1_from[:, W1_SPLIT:])
-        w1q = keep.tile([P, H], U32, name="w1q", align_bytes=64)
+        w1q = keep.tile([P, H], U32, name="w1q", tag="w1q", align_bytes=64)
         w1s = keep.tile([P, H], U8, name="w1s", align_bytes=64)
         nc.vector.quantize_mx(out=w1q[:].bitcast(FP8X4), scales=w1s[:], in_=w1_bf[:])
 
-        xw = [keep.tile([P, HALF], U32, name=f"xw{a}", align_bytes=64) for a in range(2)]
+        xw = [keep.tile([P, HALF], U32, name=f"xw{a}", tag=f"xw{a}", align_bytes=64) for a in range(2)]
         for a in range(2):
             entries = offs_sb[:, a * HALF // PER_COLUMN : (a + 1) * HALF // PER_COLUMN]
             nc.vector.tensor_copy(xw[a][:], xw_all[:].indirect(entries))
@@ -117,7 +110,21 @@ def tile_picked_devox_relu_p_kernel(
                     )
             nc.scalar.activation(h[t][:, lo:hi], h_acc[:], RELU)
 
-        for t, used_up in ((2, "w1_bf"), (3, "w1_raw")):
+        emb_rows = emb.rearrange("(p t) r -> p t r", t=PACK)
+        emb_sb = []
+        for pair, used_up in enumerate(("w1_raw", "xw_all")):
+            emb_pair = keep.tile([P, 2, U], F32, name=f"emb_pair{pair}", tag=used_up, align_bytes=64)
+            nc.sync.dma_start(emb_pair[:], emb_rows[:, 2 * pair : 2 * pair + 2, :])
+            emb_sb += [emb_pair[:, 0, :], emb_pair[:, 1, :]]
+        w2w = keep.tile([P, N], U32, name="w2w", tag="xw0", align_bytes=64)
+        w2s = keep.tile([P, N], U8, name="w2s", tag="xs", align_bytes=64)
+        gate_sb = keep.tile([P, D, V], F32, name="gate_sb", tag="w1q", align_bytes=64)
+        nc.gpsimd.memset(w2s[:].bitcast(I32), 0)
+        nc.sync.dma_start(w2w[:].bitcast(I32), w2_words[0].rearrange("p n t -> p (n t)").bitcast(I32))
+        load_scale_rows(nc.sync, w2s, w2_scales[0])
+        nc.sync.dma_start(gate_sb[:], gate.rearrange("d p v -> p d v"))
+
+        for t, used_up in ((2, "w1_bf"), (3, "xw1")):
             up.append(keep.tile([P, U], F32, name=f"up{t}", tag=used_up, align_bytes=64))
             nc.gpsimd.memset(up[t][:], 0.0)
 
@@ -128,9 +135,9 @@ def tile_picked_devox_relu_p_kernel(
             if hi < S:
                 continue
             if t < 2:
-                nc.gpsimd.tensor_tensor(early[:, t, :], up[t][:], emb_sb[t][:], ADD)
+                nc.gpsimd.tensor_tensor(early[:, t, :], up[t][:], emb_sb[t], ADD)
             elif t == 2:
-                nc.gpsimd.tensor_tensor(late[:, :, 0, :], by_128(up[t][:]), by_128(emb_sb[t][:]), ADD)
+                nc.gpsimd.tensor_tensor(late[:, :, 0, :], by_128(up[t][:]), by_128(emb_sb[t]), ADD)
         for lo, hi in LAST_ADDS:
             nc.vector.tensor_tensor(late[:, lo // P : hi // P, 1, :], by_128(up[3][:, lo:hi]), by_128(emb_sb[3][:, lo:hi]), ADD)
 

@@ -21,15 +21,16 @@ P = 128
 PACK = 4
 PER_COLUMN = 16
 HALF = S // 2
-PIECES = ((0, 0, 128), (1, 0, HALF), (0, 128, S), (1, HALF, S), (2, 0, S), (3, 0, S))
-CHUNKS = ((0, 256), (256, 512), (512, 640), (768, 1024), (640, 768))
-SCALAR_CHUNKS = 3
-LAST_ADDS = ((0, 256), (640, 1024), (256, 640))
-QUANTISE_ORDER = (3, 4, 0, 1, 2)
-OWN = 640
+PIECES = ((0, 0, 128), (1, 0, HALF), (0, 128, HALF), (1, HALF, S), (0, HALF, S), (2, 0, S), (3, 0, S))
+OWN = 704
+LAID = ((0, 256), (256, 512), (512, 640), (640, U))
+LAST_ADDS = ((0, 128), (128, 256), (OWN, U), (256, 512), (512, OWN))
+SCALAR_COPIES = ((0, 128), (128, 256), (256, 512), (512, 640), (640, OWN))
+QUANTISED = ((768, U), (0, 256), (256, 512), (512, 640), (640, 768))
+VECTOR_RELU = (256,)
 FETCH_WIDTHS = (512, 512, 128, 256)
 OUT_PARTS = ((0, 256), (256, 384), (384, 512))
-W1_SPLIT = 80
+W1_SPLIT = 92
 
 
 def load_scale_rows(queue, scale_tile, rows):
@@ -37,8 +38,10 @@ def load_scale_rows(queue, scale_tile, rows):
         queue.dma_start(scale_tile[32 * q : 32 * q + 4, :].bitcast(I32), rows[4 * q : 4 * q + 4, :].bitcast(I32))
 
 
-def by_128(ap):
-    return ap.rearrange("p (b r) -> p b r", r=P)
+def place_scale_rows(nc, queue, placed, spread):
+    nc.vector.tensor_copy(placed[:].bitcast(I32), spread[:].bitcast(I32))
+    for r in range(1, 4):
+        queue.dma_start(placed[r:P:32, :].bitcast(I32), placed[8 * r : P : 32, :].bitcast(I32))
 
 
 def tile_picked_devox_relu_p_kernel(
@@ -59,32 +62,40 @@ def tile_picked_devox_relu_p_kernel(
         up = [keep.tile([P, U], F32, name=f"up{t}") for t in range(2)]
 
         nc.gpsimd.memset(xs_all[:].bitcast(I32), 0)
+        xs = [keep.tile([P, HALF], U8, name="xs0", tag="xs0", align_bytes=64)]
         nc.vector.memset(up[0][:], 0.0)
-        nc.scalar.copy(up[1][:], up[0][:])
+        nc.vector.memset(up[1][:, : U // 2], 0.0)
+        nc.scalar.copy(up[1][:, U // 2 :], up[0][:, U // 2 :])
 
+        w1_rows = w1.rearrange("(p j) c -> p j c", j=PACK)
         nc.sync.dma_start(offs_sb[:], offs)
+        nc.scalar.dma_start(w1_raw[:, :1, :], w1_rows[:, :1, :])
         nc.sync.dma_start(cell_sb[:], cell)
         nc.sync.dma_start(xs_all[0:P:8, :].bitcast(I32), x_scales[0].bitcast(I32))
-        nc.sync.dma_start(w1_raw[:], w1.rearrange("(p j) c -> p j c", j=PACK))
+        nc.sync.dma_start(pos_sb[0][:], pos1)
+        nc.sync.dma_start(w1_raw[:, 1:, :], w1_rows[:, 1:, :])
         nc.sync.dma_start(xw_all[:].bitcast(I32), x_words[0].rearrange("p n t -> p (n t)").bitcast(I32))
-        for d, pos in enumerate((pos1, pos2, pos3, pos4)):
-            nc.sync.dma_start(pos_sb[d][:], pos)
+        for d, pos in enumerate((pos2, pos3, pos4)):
+            nc.sync.dma_start(pos_sb[d + 1][:], pos)
         make_identity(nc, ident[:])
 
-        xs_spread = keep.tile([P, S], U8, name="xs_spread", tag="xs_spread", align_bytes=64)
-        nc.vector.tensor_copy(xs_spread[:], xs_all[:].indirect(offs_sb[:]))
-        xs = keep.tile([P, S], U8, name="xs", tag="xs", align_bytes=64)
-        nc.vector.tensor_copy(xs[:].bitcast(I32), xs_spread[:].bitcast(I32))
-        for r in range(1, 4):
-            nc.scalar.dma_start(xs[r:P:32, :].bitcast(I32), xs_spread[8 * r : P : 32, :].bitcast(I32))
+        xs_spread = []
+        for a in range(2):
+            xs_spread.append(keep.tile([P, HALF], U8, name=f"xs_spread{a}", tag="xs_spread", align_bytes=64))
+            entries = offs_sb[:, a * HALF // PER_COLUMN : (a + 1) * HALF // PER_COLUMN]
+            nc.vector.tensor_copy(xs_spread[a][:], xs_all[:].indirect(entries))
+            if a == 0:
+                place_scale_rows(nc, nc.scalar, xs[0], xs_spread[0])
 
         w1_bf = keep.tile([P, PACK * P * PACK], BF16, name="w1_bf", tag="w1_bf", align_bytes=64)
         w1_to = w1_bf[:].rearrange("p (t m j) -> p m t j", t=PACK, j=PACK)
         w1_from = w1_raw[:].rearrange("p j (m t) -> p m t j", t=PACK)
         nc.vector.tensor_copy(w1_to[:, :W1_SPLIT], w1_from[:, :W1_SPLIT])
         nc.scalar.copy(w1_to[:, W1_SPLIT:], w1_from[:, W1_SPLIT:])
+        xs.append(keep.tile([P, HALF], U8, name="xs1", tag="w1_raw", align_bytes=64))
+        place_scale_rows(nc, nc.sync, xs[1], xs_spread[1])
         w1q = keep.tile([P, H], U32, name="w1q", tag="w1q", align_bytes=64)
-        w1s = keep.tile([P, H], U8, name="w1s", align_bytes=64)
+        w1s = keep.tile([P, H], U8, name="w1s", tag="w1s", align_bytes=64)
         nc.vector.quantize_mx(out=w1q[:].bitcast(FP8X4), scales=w1s[:], in_=w1_bf[:])
 
         xw = [keep.tile([P, HALF], U32, name=f"xw{a}", tag=f"xw{a}", align_bytes=64) for a in range(2)]
@@ -104,69 +115,63 @@ def tile_picked_devox_relu_p_kernel(
                         lhsT=w1q[:, plane_cols].bitcast(FP8X4),
                         lhsT_scale=w1s[:, plane_cols],
                         rhs=xw[a][:, a_lo - a * HALF : a_hi - a * HALF].bitcast(FP8X4),
-                        rhs_scale=xs[:, a_lo:a_hi],
+                        rhs_scale=xs[a][:, a_lo - a * HALF : a_hi - a * HALF],
                         start=True,
                         stop=True,
                     )
             nc.scalar.activation(h[t][:, lo:hi], h_acc[:], RELU)
 
         emb_rows = emb.rearrange("(p t) r -> p t r", t=PACK)
-        emb_sb = []
-        for pair, used_up in enumerate(("w1_raw", "xw_all")):
-            emb_pair = keep.tile([P, 2, U], F32, name=f"emb_pair{pair}", tag=used_up, align_bytes=64)
-            nc.sync.dma_start(emb_pair[:], emb_rows[:, 2 * pair : 2 * pair + 2, :])
-            emb_sb += [emb_pair[:, 0, :], emb_pair[:, 1, :]]
-        w2w = keep.tile([P, N], U32, name="w2w", tag="xw0", align_bytes=64)
-        w2s = keep.tile([P, N], U8, name="w2s", tag="xs", align_bytes=64)
-        gate_sb = keep.tile([P, D, V], F32, name="gate_sb", tag="w1q", align_bytes=64)
+        emb_early = keep.tile([P, 2, U], F32, name="emb_early", tag="xw_all", align_bytes=64)
+        nc.sync.dma_start(emb_early[:], emb_rows[:, 0:2, :])
+        late = keep.tile([P, 3, U], F32, name="late", tag="w1q", align_bytes=64)
+        nc.sync.dma_start(late[:, 1:3, :], emb_rows[:, 2:4, :])
+        w2w = keep.tile([P, N], U32, name="w2w", tag="xs_spread", align_bytes=64)
+        w2s = keep.tile([P, N], U8, name="w2s", tag="xs0", align_bytes=64)
+        gate_sb = keep.tile([P, D, V], F32, name="gate_sb", tag="w1s", align_bytes=64)
         nc.gpsimd.memset(w2s[:].bitcast(I32), 0)
         nc.sync.dma_start(w2w[:].bitcast(I32), w2_words[0].rearrange("p n t -> p (n t)").bitcast(I32))
         load_scale_rows(nc.sync, w2s, w2_scales[0])
         nc.sync.dma_start(gate_sb[:], gate.rearrange("d p v -> p d v"))
 
-        for t, used_up in ((2, "w1_bf"), (3, "xw1")):
+        for t, used_up in ((2, "xw0"), (3, "xw1")):
             up.append(keep.tile([P, U], F32, name=f"up{t}", tag=used_up, align_bytes=64))
             nc.gpsimd.memset(up[t][:], 0.0)
 
         early = keep.tile([P, 2, U], F32, name="early")
-        late = keep.tile([P, U // P, 2, P], F32, name="late")
         for t, lo, hi in PIECES:
             nc.vector.tensor_copy(up[t][:].indirect(cell_sb[:, lo // PER_COLUMN : hi // PER_COLUMN]), h[t][:, lo:hi])
             if hi < S:
                 continue
             if t < 2:
-                nc.gpsimd.tensor_tensor(early[:, t, :], up[t][:], emb_sb[t], ADD)
+                nc.gpsimd.tensor_tensor(early[:, t, :], up[t][:], emb_early[:, t, :], ADD)
             elif t == 2:
-                nc.gpsimd.tensor_tensor(late[:, :, 0, :], by_128(up[t][:]), by_128(emb_sb[t]), ADD)
-        for lo, hi in LAST_ADDS:
-            nc.vector.tensor_tensor(late[:, lo // P : hi // P, 1, :], by_128(up[3][:, lo:hi]), by_128(emb_sb[3][:, lo:hi]), ADD)
+                nc.gpsimd.tensor_tensor(late[:, 0, :], up[t][:], late[:, 1, :], ADD)
 
         y = keep.tile([P, U], F32, name="y")
-        z4 = [keep.tile([P, (hi - lo) * PACK], BF16, name=f"z4_{lo}", align_bytes=64) for lo, hi in CHUNKS]
-        for c, (lo, hi) in enumerate(CHUNKS):
-            early_to = z4[c][:].rearrange("p (r t) -> p r t", t=PACK)[:, :, 0:2]
-            nc.scalar.copy(early_to, early[:, :, lo:hi].rearrange("p t r -> p r t"))
-        for c, (lo, hi) in enumerate(CHUNKS):
-            late_to = z4[c][:].rearrange("p (b r t) -> p b r t", r=P, t=PACK)[:, :, :, 2:4]
-            late_from = late[:, lo // P : hi // P].rearrange("p b t r -> p b r t")
-            if c < SCALAR_CHUNKS:
-                nc.scalar.copy(late_to, late_from)
-            else:
-                nc.vector.tensor_copy(late_to, late_from)
+        z4 = [keep.tile([P, hi - lo, PACK], BF16, name=f"z4_{lo}", align_bytes=64) for lo, hi in LAID]
+        for c, (lo, hi) in enumerate(LAID):
+            nc.scalar.copy(z4[c][:, :, 0:2], early[:, :, lo:hi].rearrange("p t r -> p r t"))
 
-        own_acc = psum.tile([P, U - OWN], F32, name="own_acc", tag="bank3")
-        for c in QUANTISE_ORDER:
-            lo, hi = CHUNKS[c]
-            zq = keep.tile([P, hi - lo], U32, name=f"zq{c}", align_bytes=64)
-            zs = keep.tile([P, hi - lo], U8, name=f"zs{c}", align_bytes=64)
-            nc.vector.quantize_mx(out=zq[:].bitcast(FP8X4), scales=zs[:], in_=z4[c][:])
-            if c < SCALAR_CHUNKS:
-                y_acc = psum.tile([P, hi - lo], F32, name=f"yacc{c}", tag=f"bank{c}")
-                y_to = y_acc[:]
-            else:
-                y_to = own_acc[:, lo - OWN : hi - OWN]
+        def lay_late(engine_copy, lo, hi):
+            c = max(i for i, (start, end) in enumerate(LAID) if start <= lo)
+            engine_copy(z4[c][:, lo - LAID[c][0] : hi - LAID[c][0], 2:4], late[:, 0:2, lo:hi].rearrange("p t r -> p r t"))
+
+        for lo, hi in LAST_ADDS:
+            if (lo, hi) == LAST_ADDS[-1]:
+                lay_late(nc.vector.tensor_copy, OWN, U)
+            nc.vector.tensor_tensor(late[:, 1, lo:hi], up[3][:, lo:hi], late[:, 2, lo:hi], ADD)
+        for lo, hi in SCALAR_COPIES:
+            lay_late(nc.scalar.copy, lo, hi)
+
+        for bank, (lo, hi) in enumerate(QUANTISED):
+            c = max(i for i, (start, end) in enumerate(LAID) if start <= lo)
+            zq = keep.tile([P, hi - lo], U32, name=f"zq{lo}", align_bytes=64)
+            zs = keep.tile([P, hi - lo], U8, name=f"zs{lo}", align_bytes=64)
+            nc.vector.quantize_mx(out=zq[:].bitcast(FP8X4), scales=zs[:], in_=z4[c][:, lo - LAID[c][0] : hi - LAID[c][0], :].rearrange("p r t -> p (r t)"))
+            y_acc = psum.tile([P, hi - lo], F32, name=f"yacc{lo}", tag=f"bank{bank}")
             nc.tensor.matmul_mx(
-                out=y_to,
+                out=y_acc[:],
                 lhsT=w2w[:].bitcast(FP8X4),
                 lhsT_scale=w2s[:],
                 rhs=zq[:].bitcast(FP8X4),
@@ -174,9 +179,9 @@ def tile_picked_devox_relu_p_kernel(
                 start=True,
                 stop=True,
             )
-            if c == 4:
-                nc.scalar.activation(y[:, OWN:], own_acc[:], RELU)
-            elif c != 3:
+            if lo in VECTOR_RELU:
+                nc.vector.tensor_scalar_max(y[:, lo:hi], y_acc[:], 0.0)
+            else:
                 nc.scalar.activation(y[:, lo:hi], y_acc[:], RELU)
 
         terms = [keep.tile([P, V], F32, name=f"term{d}") for d in range(D)]

@@ -30,7 +30,7 @@ QUANTISED = ((768, U), (0, 256), (256, 512), (512, 640), (640, 768))
 VECTOR_RELU = (256,)
 FETCH_WIDTHS = (512, 512, 128, 256)
 OUT_PARTS = ((0, 256), (256, 384), (384, 512))
-W1_SPLIT = 92
+W1_SPLIT = 104
 
 
 def load_scale_rows(queue, scale_tile, rows):
@@ -88,8 +88,8 @@ def tile_picked_devox_relu_p_kernel(
                 place_scale_rows(nc, nc.scalar, xs[0], xs_spread[0])
 
         w1_bf = keep.tile([P, PACK * P * PACK], BF16, name="w1_bf", tag="w1_bf", align_bytes=64)
-        w1_to = w1_bf[:].rearrange("p (t m j) -> p m t j", t=PACK, j=PACK)
-        w1_from = w1_raw[:].rearrange("p j (m t) -> p m t j", t=PACK)
+        w1_to = w1_bf[:].rearrange("p (t m j) -> p m j t", t=PACK, j=PACK)
+        w1_from = w1_raw[:].rearrange("p j (m t) -> p m j t", t=PACK)
         nc.vector.tensor_copy(w1_to[:, :W1_SPLIT], w1_from[:, :W1_SPLIT])
         nc.scalar.copy(w1_to[:, W1_SPLIT:], w1_from[:, W1_SPLIT:])
         xs.append(keep.tile([P, HALF], U8, name="xs1", tag="w1_raw", align_bytes=64))

@@ -16,32 +16,20 @@ FP8X4 = mybir.dt.float8_e4m3fn_x4
 ADD = mybir.AluOpType.add
 MULT = mybir.AluOpType.mult
 RELU = mybir.ActivationFunctionType.Relu
+COPY = mybir.ActivationFunctionType.Copy
 
 P = 128
 PACK = 4
 PER_COLUMN = 16
 HALF = S // 2
-PIECES = ((0, 0, 128), (1, 0, HALF), (0, 128, HALF), (1, HALF, S), (0, HALF, S), (2, 0, S), (3, 0, S))
-OWN = 704
-LAID = ((0, 256), (256, 512), (512, 640), (640, U))
-LAST_ADDS = ((0, 128), (128, 256), (OWN, U), (256, 512), (512, OWN))
-SCALAR_COPIES = ((0, 128), (128, 256), (256, 512), (512, 640), (640, OWN))
-QUANTISED = ((768, U), (0, 256), (256, 512), (512, 640), (640, 768))
-VECTOR_RELU = (256,)
-FETCH_WIDTHS = (512, 512, 128, 256)
-OUT_PARTS = ((0, 256), (256, 384), (384, 512))
 W1_SPLIT = 104
+RANGE = 256
+SCALAR_BLOCKS = ((0, 0), (1, 0), (0, 1), (1, 1), (0, 2), (1, 2), (0, 3))
+OUT_PARTS = ((0, 256), (256, 384), (384, 512))
 
 
-def load_scale_rows(queue, scale_tile, rows):
-    for q in range(4):
-        queue.dma_start(scale_tile[32 * q : 32 * q + 4, :].bitcast(I32), rows[4 * q : 4 * q + 4, :].bitcast(I32))
-
-
-def place_scale_rows(nc, queue, placed, spread):
-    nc.vector.tensor_copy(placed[:].bitcast(I32), spread[:].bitcast(I32))
-    for r in range(1, 4):
-        queue.dma_start(placed[r:P:32, :].bitcast(I32), placed[8 * r : P : 32, :].bitcast(I32))
+def entries(list_tile, lo, hi):
+    return list_tile[:, lo // PER_COLUMN : hi // PER_COLUMN]
 
 
 def tile_picked_devox_relu_p_kernel(
@@ -55,14 +43,13 @@ def tile_picked_devox_relu_p_kernel(
         offs_sb = keep.tile([P, S // PER_COLUMN], U16, name="offs_sb")
         cell_sb = keep.tile([P, S // PER_COLUMN], U16, name="cell_sb")
         pos_sb = [keep.tile([P, V // PER_COLUMN], U16, name=f"pos_sb{d}") for d in range(D)]
-        xs_all = keep.tile([P, T], U8, name="xs_all", tag="w1_bf", align_bytes=64)
+        xs_all = keep.tile([P, T], U8, name="xs_all", align_bytes=64)
         xw_all = keep.tile([P, T], U32, name="xw_all", tag="xw_all", align_bytes=64)
         w1_raw = keep.tile([P, PACK, H], F32, name="w1_raw", tag="w1_raw", align_bytes=64)
         ident = keep.tile([P, P], F32, name="ident")
         up = [keep.tile([P, U], F32, name=f"up{t}") for t in range(2)]
 
         nc.gpsimd.memset(xs_all[:].bitcast(I32), 0)
-        xs = [keep.tile([P, HALF], U8, name="xs0", tag="xs0", align_bytes=64)]
         nc.vector.memset(up[0][:], 0.0)
         nc.vector.memset(up[1][:, : U // 2], 0.0)
         nc.scalar.copy(up[1][:, U // 2 :], up[0][:, U // 2 :])
@@ -79,97 +66,116 @@ def tile_picked_devox_relu_p_kernel(
             nc.sync.dma_start(pos_sb[d + 1][:], pos)
         make_identity(nc, ident[:])
 
-        xs_spread = []
-        for a in range(2):
-            xs_spread.append(keep.tile([P, HALF], U8, name=f"xs_spread{a}", tag="xs_spread", align_bytes=64))
-            entries = offs_sb[:, a * HALF // PER_COLUMN : (a + 1) * HALF // PER_COLUMN]
-            nc.vector.tensor_copy(xs_spread[a][:], xs_all[:].indirect(entries))
-            if a == 0:
-                place_scale_rows(nc, nc.scalar, xs[0], xs_spread[0])
+        xs_spread = keep.tile([P, S], U8, name="xs_spread", tag="xs_spread", align_bytes=64)
+        xs = keep.tile([P, S], U8, name="xs", tag="xs", align_bytes=64)
+        nc.vector.tensor_copy(xs_spread[:], xs_all[:].indirect(offs_sb[:]))
+        nc.vector.tensor_copy(xs[:].bitcast(I32), xs_spread[:].bitcast(I32))
+        for r in range(1, 4):
+            nc.scalar.dma_start(xs[r:P:32, :].bitcast(I32), xs[8 * r : P : 32, :].bitcast(I32))
 
         w1_bf = keep.tile([P, PACK * P * PACK], BF16, name="w1_bf", tag="w1_bf", align_bytes=64)
         w1_to = w1_bf[:].rearrange("p (t m j) -> p m j t", t=PACK, j=PACK)
         w1_from = w1_raw[:].rearrange("p j (m t) -> p m j t", t=PACK)
         nc.vector.tensor_copy(w1_to[:, :W1_SPLIT], w1_from[:, :W1_SPLIT])
         nc.scalar.copy(w1_to[:, W1_SPLIT:], w1_from[:, W1_SPLIT:])
-        xs.append(keep.tile([P, HALF], U8, name="xs1", tag="w1_raw", align_bytes=64))
-        place_scale_rows(nc, nc.sync, xs[1], xs_spread[1])
         w1q = keep.tile([P, H], U32, name="w1q", tag="w1q", align_bytes=64)
         w1s = keep.tile([P, H], U8, name="w1s", tag="w1s", align_bytes=64)
         nc.vector.quantize_mx(out=w1q[:].bitcast(FP8X4), scales=w1s[:], in_=w1_bf[:])
 
         xw = [keep.tile([P, HALF], U32, name=f"xw{a}", tag=f"xw{a}", align_bytes=64) for a in range(2)]
         for a in range(2):
-            entries = offs_sb[:, a * HALF // PER_COLUMN : (a + 1) * HALF // PER_COLUMN]
-            nc.vector.tensor_copy(xw[a][:], xw_all[:].indirect(entries))
-
-        h = [keep.tile([P, S], F32, name=f"h{t}") for t in range(PACK)]
-        for bank, (t, lo, hi) in enumerate(PIECES):
-            plane_cols = slice(t * P, (t + 1) * P)
-            h_acc = psum.tile([P, hi - lo], F32, name=f"acc{t}_{lo}", tag=f"bank{bank}")
-            for a in range(2):
-                a_lo, a_hi = max(lo, a * HALF), min(hi, (a + 1) * HALF)
-                if a_lo < a_hi:
-                    nc.tensor.matmul_mx(
-                        out=h_acc[:, a_lo - lo : a_hi - lo],
-                        lhsT=w1q[:, plane_cols].bitcast(FP8X4),
-                        lhsT_scale=w1s[:, plane_cols],
-                        rhs=xw[a][:, a_lo - a * HALF : a_hi - a * HALF].bitcast(FP8X4),
-                        rhs_scale=xs[a][:, a_lo - a * HALF : a_hi - a * HALF],
-                        start=True,
-                        stop=True,
-                    )
-            nc.scalar.activation(h[t][:, lo:hi], h_acc[:], RELU)
+            nc.vector.tensor_copy(xw[a][:], xw_all[:].indirect(entries(offs_sb, a * HALF, (a + 1) * HALF)))
 
         emb_rows = emb.rearrange("(p t) r -> p t r", t=PACK)
-        emb_early = keep.tile([P, 2, U], F32, name="emb_early", tag="xw_all", align_bytes=64)
-        nc.sync.dma_start(emb_early[:], emb_rows[:, 0:2, :])
-        late = keep.tile([P, 3, U], F32, name="late", tag="w1q", align_bytes=64)
-        nc.sync.dma_start(late[:, 1:3, :], emb_rows[:, 2:4, :])
-        w2w = keep.tile([P, N], U32, name="w2w", tag="xs_spread", align_bytes=64)
-        w2s = keep.tile([P, N], U8, name="w2s", tag="xs0", align_bytes=64)
-        gate_sb = keep.tile([P, D, V], F32, name="gate_sb", tag="w1s", align_bytes=64)
-        nc.gpsimd.memset(w2s[:].bitcast(I32), 0)
-        nc.sync.dma_start(w2w[:].bitcast(I32), w2_words[0].rearrange("p n t -> p (n t)").bitcast(I32))
-        load_scale_rows(nc.sync, w2s, w2_scales[0])
-        nc.sync.dma_start(gate_sb[:], gate.rearrange("d p v -> p d v"))
+        emb_sb = []
+        for u, used_up in enumerate(("w1_raw", "w1_bf")):
+            emb_sb.append(keep.tile([P, 2, U], F32, name=f"emb_sb{u}", tag=used_up, align_bytes=64))
+            nc.sync.dma_start(emb_sb[u][:], emb_rows[:, 2 * u : 2 * u + 2, :])
 
+        h = [keep.tile([P, S], F32, name=f"h{t}") for t in range(PACK)]
+        banks = {}
+
+        def product(t, lo, hi):
+            bank = len(banks)
+            banks[(t, lo)] = psum.tile([P, hi - lo], F32, name=f"acc{t}_{lo}", tag=f"bank{bank}")
+            plane_cols = slice(t * P, (t + 1) * P)
+            for a in range(lo // HALF, hi // HALF):
+                nc.tensor.matmul_mx(
+                    out=banks[(t, lo)][:, a * HALF - lo : (a + 1) * HALF - lo],
+                    lhsT=w1q[:, plane_cols].bitcast(FP8X4),
+                    lhsT_scale=w1s[:, plane_cols],
+                    rhs=xw[a][:].bitcast(FP8X4),
+                    rhs_scale=xs[:, a * HALF : (a + 1) * HALF],
+                    start=True,
+                    stop=True,
+                )
+
+        def relu_scalar(t, lo, hi):
+            nc.scalar.activation(h[t][:, lo:hi], banks[(t, lo)][:], RELU)
+
+        def scatter(t, lo, hi):
+            window = up[t][:].indirect(entries(cell_sb, lo, hi))
+            if t % 2 == 0:
+                nc.vector.tensor_copy(window, h[t][:, lo:hi])
+            else:
+                nc.scalar.activation(window, h[t][:, lo:hi], COPY)
+
+        for t, lo, hi in ((0, 0, HALF), (1, 0, HALF), (0, HALF, S), (1, HALF, S), (2, 0, S), (3, 0, S)):
+            product(t, lo, hi)
         for t, used_up in ((2, "xw0"), (3, "xw1")):
             up.append(keep.tile([P, U], F32, name=f"up{t}", tag=used_up, align_bytes=64))
             nc.gpsimd.memset(up[t][:], 0.0)
 
-        early = keep.tile([P, 2, U], F32, name="early")
-        for t, lo, hi in PIECES:
-            nc.vector.tensor_copy(up[t][:].indirect(cell_sb[:, lo // PER_COLUMN : hi // PER_COLUMN]), h[t][:, lo:hi])
-            if hi < S:
-                continue
-            if t < 2:
-                nc.gpsimd.tensor_tensor(early[:, t, :], up[t][:], emb_early[:, t, :], ADD)
-            elif t == 2:
-                nc.gpsimd.tensor_tensor(late[:, 0, :], up[t][:], late[:, 1, :], ADD)
+        w2w = keep.tile([P, N], U32, name="w2w", tag="w1q", align_bytes=64)
+        w2s = keep.tile([P, N], U8, name="w2s", tag="xs", align_bytes=64)
+        gates = keep.tile([P, 2 * V + P], F32, name="gates", tag="xw_all", align_bytes=64)
+        gate_sb = gates[:, : 2 * V].rearrange("p (d v) -> p d v", d=2)
+        gate_rest = gates[:, 2 * V :]
+        gate_t = keep.tile([P, 2, 8], F32, name="gate_t", tag="w1s", align_bytes=64)
+        nc.gpsimd.memset(w2s[:].bitcast(I32), 0)
+        nc.sync.dma_start(gate_sb, gate[2:].rearrange("d p v -> p d v"))
+        nc.sync.dma_start(w2w[:].bitcast(I32), w2_words[0].rearrange("p n t -> p (n t)").bitcast(I32))
+        for q in range(4):
+            nc.sync.dma_start(w2s[32 * q : 32 * q + 4, :].bitcast(I32), w2_scales[0][4 * q : 4 * q + 4, :].bitcast(I32))
+        with nc.allow_non_contiguous_dma(reason="one gate weight a partition"):
+            for d, blocks in ((0, 4), (1, 3)):
+                nc.sync.dma_start(gate_t[:, d, :blocks], gate[d, 0, : blocks * P].rearrange("(b p) -> p b", p=P))
+        nc.sync.dma_start(gate_rest, gate[1, :, V - P :])
+
+        relu_scalar(0, 0, HALF)
+        relu_scalar(1, 0, HALF)
+        relu_scalar(0, HALF, S)
+        scatter(0, 0, HALF)
+        scatter(1, 0, HALF)
+        nc.vector.tensor_scalar_max(h[2][:], banks[(2, 0)][:], 0.0)
+        relu_scalar(1, HALF, S)
+        relu_scalar(3, 0, S)
+        scatter(0, HALF, S)
+        scatter(1, HALF, S)
+        scatter(2, 0, S)
+        scatter(3, 0, HALF)
+        scatter(3, HALF, S)
+
+        ranges = [slice(lo, lo + RANGE) for lo in range(0, U, RANGE)]
+        pairs = [keep.tile([P, 2, RANGE, 2], BF16, name=f"pairs{c}", align_bytes=64) for c in range(len(ranges))]
+        for t in range(PACK):
+            engine = nc.gpsimd if t < 2 else nc.vector
+            for c, cells in enumerate(ranges):
+                engine.tensor_tensor(pairs[c][:, t // 2, :, t % 2], up[t][:, cells], emb_sb[t // 2][:, t % 2, cells], ADD)
 
         y = keep.tile([P, U], F32, name="y")
-        z4 = [keep.tile([P, hi - lo, PACK], BF16, name=f"z4_{lo}", align_bytes=64) for lo, hi in LAID]
-        for c, (lo, hi) in enumerate(LAID):
-            nc.scalar.copy(z4[c][:, :, 0:2], early[:, :, lo:hi].rearrange("p t r -> p r t"))
-
-        def lay_late(engine_copy, lo, hi):
-            c = max(i for i, (start, end) in enumerate(LAID) if start <= lo)
-            engine_copy(z4[c][:, lo - LAID[c][0] : hi - LAID[c][0], 2:4], late[:, 0:2, lo:hi].rearrange("p t r -> p r t"))
-
-        for lo, hi in LAST_ADDS:
-            if (lo, hi) == LAST_ADDS[-1]:
-                lay_late(nc.vector.tensor_copy, OWN, U)
-            nc.vector.tensor_tensor(late[:, 1, lo:hi], up[3][:, lo:hi], late[:, 2, lo:hi], ADD)
-        for lo, hi in SCALAR_COPIES:
-            lay_late(nc.scalar.copy, lo, hi)
-
-        for bank, (lo, hi) in enumerate(QUANTISED):
-            c = max(i for i, (start, end) in enumerate(LAID) if start <= lo)
-            zq = keep.tile([P, hi - lo], U32, name=f"zq{lo}", align_bytes=64)
-            zs = keep.tile([P, hi - lo], U8, name=f"zs{lo}", align_bytes=64)
-            nc.vector.quantize_mx(out=zq[:].bitcast(FP8X4), scales=zs[:], in_=z4[c][:, lo - LAID[c][0] : hi - LAID[c][0], :].rearrange("p r t -> p (r t)"))
-            y_acc = psum.tile([P, hi - lo], F32, name=f"yacc{lo}", tag=f"bank{bank}")
+        woven = []
+        for c in range(len(ranges)):
+            woven.append(keep.tile([P, RANGE * PACK], BF16, name=f"woven{c}", align_bytes=64))
+            nc.scalar.copy(
+                woven[c][:].bitcast(U32).rearrange("p (r u) -> p r u", u=2),
+                pairs[c][:].rearrange("p u r e -> p u (r e)").bitcast(U32).rearrange("p u r -> p r u"),
+            )
+        for c, cells in enumerate(ranges):
+            zq = keep.tile([P, RANGE], U32, name=f"zq{c}", align_bytes=64)
+            zs = keep.tile([P, RANGE], U8, name=f"zs{c}", align_bytes=64)
+            nc.vector.quantize_mx(out=zq[:].bitcast(FP8X4), scales=zs[:], in_=woven[c][:])
+            y_acc = psum.tile([P, RANGE], F32, name=f"yacc{c}", tag=f"bank{(6 + c) % 8}")
             nc.tensor.matmul_mx(
                 out=y_acc[:],
                 lhsT=w2w[:].bitcast(FP8X4),
@@ -179,33 +185,37 @@ def tile_picked_devox_relu_p_kernel(
                 start=True,
                 stop=True,
             )
-            if lo in VECTOR_RELU:
-                nc.vector.tensor_scalar_max(y[:, lo:hi], y_acc[:], 0.0)
-            else:
-                nc.scalar.activation(y[:, lo:hi], y_acc[:], RELU)
+            nc.scalar.activation(y[:, cells], y_acc[:], RELU)
 
-        terms = [keep.tile([P, V], F32, name=f"term{d}") for d in range(D)]
-        turned = [psum.tile([P, P], F32, name=f"turned{c}", tag=f"bank{c}") for c in range(V // P)]
-        sums = [psum.tile([P, hi - lo], F32, name=f"sum{lo}", tag=f"bank{5 + i}") for i, (lo, hi) in enumerate(OUT_PARTS)]
-        for d, width in enumerate(FETCH_WIDTHS):
-            for lo in range(0, V, width):
-                cols = slice(lo, lo + width)
-                entries = pos_sb[d][:, lo // PER_COLUMN : (lo + width) // PER_COLUMN]
-                nc.vector.tensor_tensor(terms[d][:, cols], y[:].indirect(entries), gate_sb[:, d, cols], MULT)
-                if d == D - 1:
-                    continue
-                for c in range(lo // P, (lo + width) // P):
-                    block = slice(c * P, (c + 1) * P)
-                    nc.tensor.matmul(
-                        turned[c][:], terms[d][:, block], ident[:], start=(d == 0), stop=(d == D - 2), is_transpose=True
-                    )
-                    if d == D - 2:
-                        summed = keep.tile([P, P], F32, name=f"summed{c}")
-                        nc.scalar.copy(summed[:], turned[c][:])
-                        part = max(0, c - 1)
-                        at = c * P - OUT_PARTS[part][0]
-                        nc.tensor.transpose(sums[part][:, at : at + P], summed[:], ident[:])
+        plain = [keep.tile([P, V], F32, name=f"plain{d}") for d in range(2)]
+        turned = {}
+        for i, (d, lo, hi) in enumerate(((0, 0, 256), (1, 0, 256), (0, 256, 512), (1, 256, 384))):
+            nc.scalar.activation(plain[d][:, lo:hi], y[:].indirect(entries(pos_sb[d], lo, hi)), COPY)
+            bank = psum.tile([P, hi - lo], F32, name=f"turned{d}_{lo}", tag=f"bank{2 + i}")
+            for b in range(lo // P, hi // P):
+                turned[(d, b)] = bank[:, b * P - lo : (b + 1) * P - lo]
+                nc.tensor.transpose(turned[(d, b)], plain[d][:, b * P : (b + 1) * P], ident[:])
+        sums = [psum.tile([P, hi - lo], F32, name=f"sum{lo}", tag=f"bank{(6 + i) % 8}") for i, (lo, hi) in enumerate(OUT_PARTS)]
+        for d, b in SCALAR_BLOCKS:
+            weighted = keep.tile([P, P], F32, name=f"weighted{d}_{b}")
+            nc.scalar.activation(weighted[:], turned[(d, b)], COPY, scale=gate_t[:, d, b : b + 1])
+            part = max(0, b - 1)
+            at = b * P - OUT_PARTS[part][0]
+            nc.tensor.matmul(
+                sums[part][:, at : at + P], weighted[:], ident[:], start=(d == 0), stop=(d == 1 or b == 3), is_transpose=True
+            )
+
+        terms = [keep.tile([P, V], F32, name=f"term{d}") for d in range(2)]
+        rest = keep.tile([P, P], F32, name="rest")
+        last = slice(V - P, V)
+        nc.vector.tensor_tensor(terms[0][:], y[:].indirect(pos_sb[2][:]), gate_sb[:, 0, :], MULT)
+        nc.vector.tensor_tensor(rest[:], y[:].indirect(entries(pos_sb[1], V - P, V)), gate_rest, MULT)
+        nc.vector.tensor_tensor(terms[1][:, :256], y[:].indirect(entries(pos_sb[3], 0, 256)), gate_sb[:, 1, :256], MULT)
+        nc.vector.tensor_tensor(terms[0][:, last], terms[0][:, last], rest[:], ADD)
+        nc.vector.tensor_tensor(terms[1][:, 256:], y[:].indirect(entries(pos_sb[3], 256, V)), gate_sb[:, 1, 256:], MULT)
+        for lo in (0, 256):
+            nc.vector.tensor_tensor(terms[0][:, lo : lo + 256], terms[0][:, lo : lo + 256], terms[1][:, lo : lo + 256], ADD)
         for (lo, hi), part_sum, queue in zip(OUT_PARTS, sums, (nc.sync, nc.scalar, nc.sync)):
             res = keep.tile([P, hi - lo], F32, name=f"res{lo}")
-            nc.vector.tensor_tensor(res[:], part_sum[:], terms[D - 1][:, lo:hi], ADD)
+            nc.vector.tensor_tensor(res[:], part_sum[:], terms[0][:, lo:hi], ADD)
             queue.dma_start(out[:, lo:hi], res[:])

@@ -23,8 +23,11 @@ PACK = 4
 PER_COLUMN = 16
 HALF = S // 2
 W1_SPLIT = 104
-RANGE = 256
-SCALAR_BLOCKS = ((0, 0), (1, 0), (0, 1), (1, 1), (0, 2), (1, 2), (0, 3))
+RANGES = ((512, 768), (768, 1024), (0, 256), (256, 384), (384, 512))
+TURNED = 512
+Y_BANKS = {512: 7, 768: 0, 0: 4, 256: 5, 384: 6}
+VECTOR_RELU = (256, 384)
+ADDS = ((0, 512, 1024), (1, 512, 1024), (2, 512, 1024), (3, 512, 768), (3, 768, 1024))
 OUT_PARTS = ((0, 256), (256, 384), (384, 512))
 
 
@@ -47,12 +50,13 @@ def tile_picked_devox_relu_p_kernel(
         xw_all = keep.tile([P, T], U32, name="xw_all", tag="xw_all", align_bytes=64)
         w1_raw = keep.tile([P, PACK, H], F32, name="w1_raw", tag="w1_raw", align_bytes=64)
         ident = keep.tile([P, P], F32, name="ident")
-        up = [keep.tile([P, U], F32, name=f"up{t}") for t in range(2)]
+        up = [keep.tile([P, U], F32, name=f"up{t}") for t in range(PACK)]
 
         nc.gpsimd.memset(xs_all[:].bitcast(I32), 0)
-        nc.vector.memset(up[0][:], 0.0)
-        nc.vector.memset(up[1][:, : U // 2], 0.0)
-        nc.scalar.copy(up[1][:, U // 2 :], up[0][:, U // 2 :])
+        nc.vector.memset(up[0][:].bitcast(I32), 0)
+        nc.scalar.copy(up[1][:], up[0][:])
+        for t in (2, 3):
+            nc.vector.tensor_copy(up[t][:], up[0][:])
 
         w1_rows = w1.rearrange("(p j) c -> p j c", j=PACK)
         nc.sync.dma_start(offs_sb[:], offs)
@@ -86,18 +90,12 @@ def tile_picked_devox_relu_p_kernel(
         for a in range(2):
             nc.vector.tensor_copy(xw[a][:], xw_all[:].indirect(entries(offs_sb, a * HALF, (a + 1) * HALF)))
 
-        emb_rows = emb.rearrange("(p t) r -> p t r", t=PACK)
-        emb_sb = []
-        for u, used_up in enumerate(("w1_raw", "w1_bf")):
-            emb_sb.append(keep.tile([P, 2, U], F32, name=f"emb_sb{u}", tag=used_up, align_bytes=64))
-            nc.sync.dma_start(emb_sb[u][:], emb_rows[:, 2 * u : 2 * u + 2, :])
-
         h = [keep.tile([P, S], F32, name=f"h{t}") for t in range(PACK)]
         banks = {}
 
         def product(t, lo, hi):
             bank = len(banks)
-            banks[(t, lo)] = psum.tile([P, hi - lo], F32, name=f"acc{t}_{lo}", tag=f"bank{bank}")
+            banks[(t, lo)] = psum.tile([P, hi - lo], F32, name=f"acc{t}_{lo}", tag=f"bank{bank % 4}")
             plane_cols = slice(t * P, (t + 1) * P)
             for a in range(lo // HALF, hi // HALF):
                 nc.tensor.matmul_mx(
@@ -113,6 +111,9 @@ def tile_picked_devox_relu_p_kernel(
         def relu_scalar(t, lo, hi):
             nc.scalar.activation(h[t][:, lo:hi], banks[(t, lo)][:], RELU)
 
+        def relu_vector(t, lo, hi):
+            nc.vector.tensor_scalar_max(h[t][:, lo:hi], banks[(t, lo)][:], 0.0)
+
         def scatter(t, lo, hi):
             window = up[t][:].indirect(entries(cell_sb, lo, hi))
             if t % 2 == 0:
@@ -120,62 +121,92 @@ def tile_picked_devox_relu_p_kernel(
             else:
                 nc.scalar.activation(window, h[t][:, lo:hi], COPY)
 
-        for t, lo, hi in ((0, 0, HALF), (1, 0, HALF), (0, HALF, S), (1, HALF, S), (2, 0, S), (3, 0, S)):
-            product(t, lo, hi)
-        for t, used_up in ((2, "xw0"), (3, "xw1")):
-            up.append(keep.tile([P, U], F32, name=f"up{t}", tag=used_up, align_bytes=64))
-            nc.gpsimd.memset(up[t][:], 0.0)
+        for lo in (0, HALF):
+            for t in range(PACK):
+                product(t, lo, lo + HALF)
+
+        emb_rows = emb.rearrange("(p t) r -> p t r", t=PACK)
+        emb_sb = []
+        for u, used_up in enumerate(("xw_all", "xw0")):
+            emb_sb.append(keep.tile([P, 2, U], F32, name=f"emb_sb{u}", tag=used_up, align_bytes=64))
+            nc.sync.dma_start(emb_sb[u][:], emb_rows[:, 2 * u : 2 * u + 2, :])
 
         w2w = keep.tile([P, N], U32, name="w2w", tag="w1q", align_bytes=64)
         w2s = keep.tile([P, N], U8, name="w2s", tag="xs", align_bytes=64)
-        gates = keep.tile([P, 2 * V + P], F32, name="gates", tag="xw_all", align_bytes=64)
-        gate_sb = gates[:, : 2 * V].rearrange("p (d v) -> p d v", d=2)
-        gate_rest = gates[:, 2 * V :]
-        gate_t = keep.tile([P, 2, 8], F32, name="gate_t", tag="w1s", align_bytes=64)
+        gate_sb = keep.tile([P, D - 1, V], F32, name="gate_sb", tag="xw1", align_bytes=64)
+        gate_t = keep.tile([P, V // P], F32, name="gate_t", tag="w1s", align_bytes=64)
         nc.gpsimd.memset(w2s[:].bitcast(I32), 0)
-        nc.sync.dma_start(gate_sb, gate[2:].rearrange("d p v -> p d v"))
         nc.sync.dma_start(w2w[:].bitcast(I32), w2_words[0].rearrange("p n t -> p (n t)").bitcast(I32))
         for q in range(4):
             nc.sync.dma_start(w2s[32 * q : 32 * q + 4, :].bitcast(I32), w2_scales[0][4 * q : 4 * q + 4, :].bitcast(I32))
         with nc.allow_non_contiguous_dma(reason="one gate weight a partition"):
-            for d, blocks in ((0, 4), (1, 3)):
-                nc.sync.dma_start(gate_t[:, d, :blocks], gate[d, 0, : blocks * P].rearrange("(b p) -> p b", p=P))
-        nc.sync.dma_start(gate_rest, gate[1, :, V - P :])
+            nc.sync.dma_start(gate_t[:], gate[0, 0, :].rearrange("(b p) -> p b", p=P))
+        nc.sync.dma_start(gate_sb[:], gate[1:].rearrange("d p v -> p d v"))
 
-        relu_scalar(0, 0, HALF)
-        relu_scalar(1, 0, HALF)
-        relu_scalar(0, HALF, S)
+        for t in (0, 1, 2):
+            relu_scalar(t, 0, HALF)
         scatter(0, 0, HALF)
         scatter(1, 0, HALF)
-        nc.vector.tensor_scalar_max(h[2][:], banks[(2, 0)][:], 0.0)
-        relu_scalar(1, HALF, S)
-        relu_scalar(3, 0, S)
-        scatter(0, HALF, S)
-        scatter(1, HALF, S)
-        scatter(2, 0, S)
+        scatter(2, 0, HALF)
+        relu_scalar(3, 0, HALF)
+        relu_scalar(0, HALF, S)
+        relu_vector(1, HALF, S)
         scatter(3, 0, HALF)
+        scatter(0, HALF, S)
+        relu_vector(2, HALF, S)
+        relu_scalar(3, HALF, S)
+        scatter(1, HALF, S)
+        scatter(2, HALF, S)
         scatter(3, HALF, S)
 
-        ranges = [slice(lo, lo + RANGE) for lo in range(0, U, RANGE)]
-        pairs = [keep.tile([P, 2, RANGE, 2], BF16, name=f"pairs{c}", align_bytes=64) for c in range(len(ranges))]
-        for t in range(PACK):
-            engine = nc.gpsimd if t < 2 else nc.vector
-            for c, cells in enumerate(ranges):
-                engine.tensor_tensor(pairs[c][:, t // 2, :, t % 2], up[t][:, cells], emb_sb[t // 2][:, t % 2, cells], ADD)
+        groups = range(TURNED // HALF)
+        z_t = [[psum.tile([P, 2, 2, P], F32, name=f"z_t{u}{g}", tag=f"bank{4 + 2 * u + g}") for g in groups] for u in range(2)]
+        for u in range(2):
+            sources = [emb_sb[u][:, e, :] for e in range(2)] + [up[2 * u + e][:] for e in range(2)]
+            for i, source in enumerate(sources):
+                for g in groups:
+                    for b in range(2):
+                        cells = slice(g * HALF + b * P, g * HALF + (b + 1) * P)
+                        first, final = (i, b) == (0, 0), (i, b) == (3, 1)
+                        nc.tensor.matmul(
+                            z_t[u][g][:, b, i % 2, :], source[:, cells], ident[:], start=first, stop=final, is_transpose=True
+                        )
+        z = keep.tile([P, PACK, U - TURNED], BF16, name="z")
+        for t, lo, hi in ADDS:
+            nc.vector.tensor_tensor(z[:, t, lo - TURNED : hi - TURNED], up[t][:, lo:hi], emb_sb[t // 2][:, t % 2, lo:hi], ADD)
 
         y = keep.tile([P, U], F32, name="y")
-        woven = []
-        for c in range(len(ranges)):
-            woven.append(keep.tile([P, RANGE * PACK], BF16, name=f"woven{c}", align_bytes=64))
-            nc.scalar.copy(
-                woven[c][:].bitcast(U32).rearrange("p (r u) -> p r u", u=2),
-                pairs[c][:].rearrange("p u r e -> p u (r e)").bitcast(U32).rearrange("p u r -> p r u"),
-            )
-        for c, cells in enumerate(ranges):
-            zq = keep.tile([P, RANGE], U32, name=f"zq{c}", align_bytes=64)
-            zs = keep.tile([P, RANGE], U8, name=f"zs{c}", align_bytes=64)
-            nc.vector.quantize_mx(out=zq[:].bitcast(FP8X4), scales=zs[:], in_=woven[c][:])
-            y_acc = psum.tile([P, RANGE], F32, name=f"yacc{c}", tag=f"bank{(6 + c) % 8}")
+        woven = {}
+        rounded = []
+        for u in range(2):
+            rounded.append([keep.tile([P, 2 * P * 2], BF16, name=f"rounded{u}{g}", align_bytes=64) for g in groups])
+            for g in groups:
+                nc.scalar.copy(
+                    rounded[u][g][:].rearrange("r (b p e) -> r b p e", b=2, e=2), z_t[u][g][:].rearrange("r b e p -> r b p e")
+                )
+        for lo, hi in RANGES:
+            woven[lo] = keep.tile([P, (hi - lo) * PACK], BF16, name=f"woven{lo}", align_bytes=64)
+            if lo >= TURNED:
+                nc.vector.tensor_copy(
+                    woven[lo][:].rearrange("p (r t) -> p r t", t=PACK),
+                    z[:, :, lo - TURNED : hi - TURNED].rearrange("p t r -> p r t"),
+                )
+            else:
+                back = psum.tile([P, 2, hi - lo], F32, name=f"back{lo}", tag=f"bank{max(0, lo // P - 1)}")
+                for u in range(2):
+                    for b in range(lo // P, hi // P):
+                        at = b * P - lo
+                        words = rounded[u][b // 2][:].bitcast(F32)[:, (b % 2) * P : (b % 2 + 1) * P]
+                        nc.tensor.transpose(back[:, u, at : at + P], words, ident[:])
+                nc.scalar.copy(woven[lo][:].bitcast(F32).rearrange("p (r u) -> p r u", u=2), back[:].rearrange("p u r -> p r u"))
+        late = []
+        for lo, hi in RANGES:
+            width = hi - lo
+            zq = keep.tile([P, width], U32, name=f"zq{lo}", align_bytes=64)
+            zs = keep.tile([P, width], U8, name=f"zs{lo}", align_bytes=64)
+            nc.vector.quantize_mx(out=zq[:].bitcast(FP8X4), scales=zs[:], in_=woven[lo][:])
+            bank = Y_BANKS[lo]
+            y_acc = psum.tile([P, width], F32, name=f"yacc{lo}", tag=f"bank{bank}")
             nc.tensor.matmul_mx(
                 out=y_acc[:],
                 lhsT=w2w[:].bitcast(FP8X4),
@@ -185,37 +216,54 @@ def tile_picked_devox_relu_p_kernel(
                 start=True,
                 stop=True,
             )
-            nc.scalar.activation(y[:, cells], y_acc[:], RELU)
+            if lo in VECTOR_RELU:
+                late.append((slice(lo, hi), y_acc))
+            else:
+                nc.scalar.activation(y[:, lo:hi], y_acc[:], RELU)
+        for cells, y_acc in late:
+            nc.vector.tensor_scalar_max(y[:, cells], y_acc[:], 0.0)
 
-        plain = [keep.tile([P, V], F32, name=f"plain{d}") for d in range(2)]
-        turned = {}
-        for i, (d, lo, hi) in enumerate(((0, 0, 256), (1, 0, 256), (0, 256, 512), (1, 256, 384))):
-            nc.scalar.activation(plain[d][:, lo:hi], y[:].indirect(entries(pos_sb[d], lo, hi)), COPY)
-            bank = psum.tile([P, hi - lo], F32, name=f"turned{d}_{lo}", tag=f"bank{2 + i}")
-            for b in range(lo // P, hi // P):
-                turned[(d, b)] = bank[:, b * P - lo : (b + 1) * P - lo]
-                nc.tensor.transpose(turned[(d, b)], plain[d][:, b * P : (b + 1) * P], ident[:])
-        sums = [psum.tile([P, hi - lo], F32, name=f"sum{lo}", tag=f"bank{(6 + i) % 8}") for i, (lo, hi) in enumerate(OUT_PARTS)]
-        for d, b in SCALAR_BLOCKS:
-            weighted = keep.tile([P, P], F32, name=f"weighted{d}_{b}")
-            nc.scalar.activation(weighted[:], turned[(d, b)], COPY, scale=gate_t[:, d, b : b + 1])
+        plain = keep.tile([P, V], F32, name="plain")
+        turned = []
+        for a in range(2):
+            cols = slice(a * HALF, (a + 1) * HALF)
+            nc.scalar.activation(plain[:, cols], y[:].indirect(entries(pos_sb[0], a * HALF, (a + 1) * HALF)), COPY)
+            turned.append(psum.tile([P, 2, P], F32, name=f"turned{a}", tag=f"bank{(3, 1)[a]}"))
+            for b in range(2):
+                nc.tensor.transpose(turned[a][:, b, :], plain[:, a * HALF + b * P : a * HALF + (b + 1) * P], ident[:])
+        terms = [keep.tile([P, V], F32, name=f"term{d}") for d in range(3)]
+        both = [psum.tile([P, 2, P], F32, name=f"both{a}", tag=f"bank{(2, 7)[a]}") for a in range(2)]
+        for d, width in ((0, V), (1, HALF), (2, HALF)):
+            for lo in range(0, V, width):
+                cols = slice(lo, lo + width)
+                nc.vector.tensor_tensor(terms[d][:, cols], y[:].indirect(entries(pos_sb[d + 1], lo, lo + width)), gate_sb[:, d, cols], MULT)
+                if d < 2:
+                    for b in range(lo // P, (lo + width) // P):
+                        nc.tensor.matmul(
+                            both[b // 2][:, b % 2, :],
+                            terms[d][:, b * P : (b + 1) * P],
+                            ident[:],
+                            start=(d == 0 and b % 2 == 0),
+                            stop=(d == 1 and b % 2 == 1),
+                            is_transpose=True,
+                        )
+        sums = [psum.tile([P, hi - lo], F32, name=f"sum{lo}", tag=f"bank{(0, 4, 5)[i]}") for i, (lo, hi) in enumerate(OUT_PARTS)]
+
+        def turn_back(source, b, start, stop):
             part = max(0, b - 1)
             at = b * P - OUT_PARTS[part][0]
-            nc.tensor.matmul(
-                sums[part][:, at : at + P], weighted[:], ident[:], start=(d == 0), stop=(d == 1 or b == 3), is_transpose=True
-            )
+            nc.tensor.matmul(sums[part][:, at : at + P], source, ident[:], start=start, stop=stop, is_transpose=True)
 
-        terms = [keep.tile([P, V], F32, name=f"term{d}") for d in range(2)]
-        rest = keep.tile([P, P], F32, name="rest")
-        last = slice(V - P, V)
-        nc.vector.tensor_tensor(terms[0][:], y[:].indirect(pos_sb[2][:]), gate_sb[:, 0, :], MULT)
-        nc.vector.tensor_tensor(rest[:], y[:].indirect(entries(pos_sb[1], V - P, V)), gate_rest, MULT)
-        nc.vector.tensor_tensor(terms[1][:, :256], y[:].indirect(entries(pos_sb[3], 0, 256)), gate_sb[:, 1, :256], MULT)
-        nc.vector.tensor_tensor(terms[0][:, last], terms[0][:, last], rest[:], ADD)
-        nc.vector.tensor_tensor(terms[1][:, 256:], y[:].indirect(entries(pos_sb[3], 256, V)), gate_sb[:, 1, 256:], MULT)
-        for lo in (0, 256):
-            nc.vector.tensor_tensor(terms[0][:, lo : lo + 256], terms[0][:, lo : lo + 256], terms[1][:, lo : lo + 256], ADD)
+        for b in range(V // P):
+            weighted = keep.tile([P, P], F32, name=f"weighted{b}")
+            nc.scalar.activation(weighted[:], turned[b // 2][:, b % 2, :], COPY, scale=gate_t[:, b : b + 1])
+            turn_back(weighted[:], b, b != 1, False)
+        for a in range(2):
+            carried = keep.tile([P, 2, P], F32, name=f"carried{a}")
+            nc.scalar.copy(carried[:], both[a][:])
+            for b in range(2):
+                turn_back(carried[:, b, :], 2 * a + b, False, 2 * a + b != 0)
         for (lo, hi), part_sum, queue in zip(OUT_PARTS, sums, (nc.sync, nc.scalar, nc.sync)):
             res = keep.tile([P, hi - lo], F32, name=f"res{lo}")
-            nc.vector.tensor_tensor(res[:], part_sum[:], terms[0][:, lo:hi], ADD)
+            nc.vector.tensor_tensor(res[:], part_sum[:], terms[2][:, lo:hi], ADD)
             queue.dma_start(out[:, lo:hi], res[:])

@@ -23,6 +23,7 @@ PACK = 4
 PER_COLUMN = 16
 HALF = S // 2
 W1_SPLIT = 104
+WORD_PIECES = ((0, 128), (128, 256), (256, 512))
 RANGES = ((512, 768), (768, 1024), (0, 256), (256, 384), (384, 512))
 TURNED = 512
 Y_BANKS = {512: 7, 768: 0, 0: 4, 256: 5, 384: 6}
@@ -63,11 +64,10 @@ def tile_picked_devox_relu_p_kernel(
         nc.scalar.dma_start(w1_raw[:, :1, :], w1_rows[:, :1, :])
         nc.sync.dma_start(cell_sb[:], cell)
         nc.sync.dma_start(xs_all[0:P:8, :].bitcast(I32), x_scales[0].bitcast(I32))
-        nc.sync.dma_start(pos_sb[0][:], pos1)
         nc.sync.dma_start(w1_raw[:, 1:, :], w1_rows[:, 1:, :])
         nc.sync.dma_start(xw_all[:].bitcast(I32), x_words[0].rearrange("p n t -> p (n t)").bitcast(I32))
-        for d, pos in enumerate((pos2, pos3, pos4)):
-            nc.sync.dma_start(pos_sb[d + 1][:], pos)
+        for d, pos in enumerate((pos1, pos2, pos3, pos4)):
+            nc.sync.dma_start(pos_sb[d][:], pos)
         make_identity(nc, ident[:])
 
         xs_spread = keep.tile([P, S], U8, name="xs_spread", tag="xs_spread", align_bytes=64)
@@ -87,26 +87,28 @@ def tile_picked_devox_relu_p_kernel(
         nc.vector.quantize_mx(out=w1q[:].bitcast(FP8X4), scales=w1s[:], in_=w1_bf[:])
 
         xw = [keep.tile([P, HALF], U32, name=f"xw{a}", tag=f"xw{a}", align_bytes=64) for a in range(2)]
-        for a in range(2):
-            nc.vector.tensor_copy(xw[a][:], xw_all[:].indirect(entries(offs_sb, a * HALF, (a + 1) * HALF)))
+        for lo, hi in WORD_PIECES:
+            a = lo // HALF
+            nc.vector.tensor_copy(xw[a][:, lo - a * HALF : hi - a * HALF], xw_all[:].indirect(entries(offs_sb, lo, hi)))
 
         h = [keep.tile([P, S], F32, name=f"h{t}") for t in range(PACK)]
         banks = {}
 
         def product(t, lo, hi):
-            bank = len(banks)
-            banks[(t, lo)] = psum.tile([P, hi - lo], F32, name=f"acc{t}_{lo}", tag=f"bank{bank % 4}")
+            a = lo // HALF
+            first = a * HALF
+            if lo == first:
+                banks[(t, first)] = psum.tile([P, HALF], F32, name=f"acc{t}_{lo}", tag=f"bank{len(banks) % 4}")
             plane_cols = slice(t * P, (t + 1) * P)
-            for a in range(lo // HALF, hi // HALF):
-                nc.tensor.matmul_mx(
-                    out=banks[(t, lo)][:, a * HALF - lo : (a + 1) * HALF - lo],
-                    lhsT=w1q[:, plane_cols].bitcast(FP8X4),
-                    lhsT_scale=w1s[:, plane_cols],
-                    rhs=xw[a][:].bitcast(FP8X4),
-                    rhs_scale=xs[:, a * HALF : (a + 1) * HALF],
-                    start=True,
-                    stop=True,
-                )
+            nc.tensor.matmul_mx(
+                out=banks[(t, first)][:, lo - first : hi - first],
+                lhsT=w1q[:, plane_cols].bitcast(FP8X4),
+                lhsT_scale=w1s[:, plane_cols],
+                rhs=xw[a][:, lo - first : hi - first].bitcast(FP8X4),
+                rhs_scale=xs[:, lo:hi],
+                start=True,
+                stop=True,
+            )
 
         def relu_scalar(t, lo, hi):
             nc.scalar.activation(h[t][:, lo:hi], banks[(t, lo)][:], RELU)
@@ -121,9 +123,11 @@ def tile_picked_devox_relu_p_kernel(
             else:
                 nc.scalar.activation(window, h[t][:, lo:hi], COPY)
 
-        for lo in (0, HALF):
-            for t in range(PACK):
-                product(t, lo, lo + HALF)
+        for lo in (0, P):
+            for t in range(2):
+                product(t, lo, lo + P)
+        for t, a in ((2, 0), (0, 1), (2, 1), (3, 0), (1, 1), (3, 1)):
+            product(t, a * HALF, (a + 1) * HALF)
 
         emb_rows = emb.rearrange("(p t) r -> p t r", t=PACK)
         emb_sb = []
@@ -147,16 +151,15 @@ def tile_picked_devox_relu_p_kernel(
             relu_scalar(t, 0, HALF)
         scatter(0, 0, HALF)
         scatter(1, 0, HALF)
-        scatter(2, 0, HALF)
-        relu_scalar(3, 0, HALF)
-        relu_scalar(0, HALF, S)
-        relu_vector(1, HALF, S)
-        scatter(3, 0, HALF)
-        scatter(0, HALF, S)
+        relu_vector(0, HALF, S)
         relu_vector(2, HALF, S)
+        scatter(0, HALF, S)
+        relu_scalar(3, 0, HALF)
+        relu_scalar(1, HALF, S)
+        scatter(3, 0, HALF)
         relu_scalar(3, HALF, S)
+        scatter(2, 0, S)
         scatter(1, HALF, S)
-        scatter(2, HALF, S)
         scatter(3, HALF, S)
 
         groups = range(TURNED // HALF)
@@ -171,9 +174,10 @@ def tile_picked_devox_relu_p_kernel(
                         nc.tensor.matmul(
                             z_t[u][g][:, b, i % 2, :], source[:, cells], ident[:], start=first, stop=final, is_transpose=True
                         )
-        z = keep.tile([P, PACK, U - TURNED], BF16, name="z")
+        z = keep.tile([P, PACK, U - TURNED], F32, name="z")
         for t, lo, hi in ADDS:
-            nc.vector.tensor_tensor(z[:, t, lo - TURNED : hi - TURNED], up[t][:, lo:hi], emb_sb[t // 2][:, t % 2, lo:hi], ADD)
+            engine = nc.gpsimd if t < 2 else nc.vector
+            engine.tensor_tensor(z[:, t, lo - TURNED : hi - TURNED], up[t][:, lo:hi], emb_sb[t // 2][:, t % 2, lo:hi], ADD)
 
         y = keep.tile([P, U], F32, name="y")
         woven = {}
@@ -181,7 +185,8 @@ def tile_picked_devox_relu_p_kernel(
         for u in range(2):
             rounded.append([keep.tile([P, 2 * P * 2], BF16, name=f"rounded{u}{g}", align_bytes=64) for g in groups])
             for g in groups:
-                nc.scalar.copy(
+                round_out = nc.vector.tensor_copy if (u, g) == (0, 1) else nc.scalar.copy
+                round_out(
                     rounded[u][g][:].rearrange("r (b p e) -> r b p e", b=2, e=2), z_t[u][g][:].rearrange("r b e p -> r b p e")
                 )
         for lo, hi in RANGES:

@@ -26,6 +26,7 @@ W1_SPLIT = 104
 WORD_PIECES = ((0, 128), (128, 256), (256, 512))
 RANGES = ((512, 768), (768, 1024), (0, 256), (256, 384), (384, 512))
 TURNED = 512
+FIRST = 128
 Y_BANKS = {512: 7, 768: 0, 0: 4, 256: 5, 384: 6}
 VECTOR_RELU = (256, 384)
 ADDS = ((0, 512, 1024), (1, 512, 1024), (2, 512, 1024), (3, 512, 768), (3, 768, 1024))
@@ -91,43 +92,52 @@ def tile_picked_devox_relu_p_kernel(
             a = lo // HALF
             nc.vector.tensor_copy(xw[a][:, lo - a * HALF : hi - a * HALF], xw_all[:].indirect(entries(offs_sb, lo, hi)))
 
-        h = [keep.tile([P, S], F32, name=f"h{t}") for t in range(PACK)]
-        banks = {}
+        h_first = keep.tile([P, 2, FIRST], F32, name="h_first")
+        h_rest = [keep.tile([P, 2 * S - FIRST], F32, name=f"h_rest{e}") for e in range(2)]
+        later = S - FIRST
 
-        def product(t, lo, hi):
+        def product(to, t, lo, hi):
             a = lo // HALF
-            first = a * HALF
-            if lo == first:
-                banks[(t, first)] = psum.tile([P, HALF], F32, name=f"acc{t}_{lo}", tag=f"bank{len(banks) % 4}")
             plane_cols = slice(t * P, (t + 1) * P)
             nc.tensor.matmul_mx(
-                out=banks[(t, first)][:, lo - first : hi - first],
+                out=to,
                 lhsT=w1q[:, plane_cols].bitcast(FP8X4),
                 lhsT_scale=w1s[:, plane_cols],
-                rhs=xw[a][:, lo - first : hi - first].bitcast(FP8X4),
+                rhs=xw[a][:, lo - a * HALF : hi - a * HALF].bitcast(FP8X4),
                 rhs_scale=xs[:, lo:hi],
                 start=True,
                 stop=True,
             )
 
-        def relu_scalar(t, lo, hi):
-            nc.scalar.activation(h[t][:, lo:hi], banks[(t, lo)][:], RELU)
+        def relu(e, to, acc):
+            if e == 0:
+                nc.vector.tensor_scalar_max(to, acc, 0.0)
+            else:
+                nc.scalar.activation(to, acc, RELU)
 
-        def relu_vector(t, lo, hi):
-            nc.vector.tensor_scalar_max(h[t][:, lo:hi], banks[(t, lo)][:], 0.0)
-
-        def scatter(t, lo, hi):
+        def scatter(t, lo, hi, values):
             window = up[t][:].indirect(entries(cell_sb, lo, hi))
             if t % 2 == 0:
-                nc.vector.tensor_copy(window, h[t][:, lo:hi])
+                nc.vector.tensor_copy(window, values)
             else:
-                nc.scalar.activation(window, h[t][:, lo:hi], COPY)
+                nc.scalar.activation(window, values, COPY)
 
-        for lo in (0, P):
-            for t in range(2):
-                product(t, lo, lo + P)
-        for t, a in ((2, 0), (0, 1), (2, 1), (3, 0), (1, 1), (3, 1)):
-            product(t, a * HALF, (a + 1) * HALF)
+        first = psum.tile([P, 2, FIRST], F32, name="first", tag="bank0")
+        for e in range(2):
+            product(first[:, e, :], e, 0, FIRST)
+        relu(1, h_first[:], first[:])
+        for e in range(2):
+            second = psum.tile([P, FIRST], F32, name=f"second{e}", tag=f"bank{(3, 1)[e]}")
+            product(second[:], e, FIRST, HALF)
+            relu(e, h_rest[e][:, :FIRST], second[:])
+        mixed = [psum.tile([P, S], F32, name=f"mixed{e}", tag=f"bank{(2, 0)[e]}") for e in range(2)]
+        last = [psum.tile([P, HALF], F32, name=f"last{e}", tag=f"bank{(3, 1)[e]}") for e in range(2)]
+        product(mixed[0][:, HALF:], 2, 0, HALF)
+        product(mixed[0][:, :HALF], 0, HALF, S)
+        product(mixed[1][:, HALF:], 3, 0, HALF)
+        product(mixed[1][:, :HALF], 1, HALF, S)
+        for e in range(2):
+            product(last[e][:], 2 + e, HALF, S)
 
         emb_rows = emb.rearrange("(p t) r -> p t r", t=PACK)
         emb_sb = []
@@ -147,20 +157,19 @@ def tile_picked_devox_relu_p_kernel(
             nc.sync.dma_start(gate_t[:], gate[0, 0, :].rearrange("(b p) -> p b", p=P))
         nc.sync.dma_start(gate_sb[:], gate[1:].rearrange("d p v -> p d v"))
 
-        for t in (0, 1, 2):
-            relu_scalar(t, 0, HALF)
-        scatter(0, 0, HALF)
-        scatter(1, 0, HALF)
-        relu_vector(0, HALF, S)
-        relu_vector(2, HALF, S)
-        scatter(0, HALF, S)
-        relu_scalar(3, 0, HALF)
-        relu_scalar(1, HALF, S)
-        scatter(3, 0, HALF)
-        relu_scalar(3, HALF, S)
-        scatter(2, 0, S)
-        scatter(1, HALF, S)
-        scatter(3, HALF, S)
+        scatter(0, 0, FIRST, h_first[:, 0, :])
+        relu(0, h_rest[0][:, FIRST:later], mixed[0][:, :HALF])
+        relu(0, h_rest[0][:, later : later + HALF], mixed[0][:, HALF:])
+        scatter(0, FIRST, S, h_rest[0][:, :later])
+        scatter(1, 0, FIRST, h_first[:, 1, :])
+        relu(1, h_rest[1][:, later : later + HALF], mixed[1][:, HALF:])
+        relu(1, h_rest[1][:, FIRST:later], mixed[1][:, :HALF])
+        scatter(3, 0, HALF, h_rest[1][:, later : later + HALF])
+        relu(1, h_rest[0][:, FIRST + S :], last[0][:])
+        relu(1, h_rest[1][:, FIRST + S :], last[1][:])
+        scatter(2, 0, S, h_rest[0][:, later:])
+        scatter(1, FIRST, S, h_rest[1][:, :later])
+        scatter(3, HALF, S, h_rest[1][:, later + HALF :])
 
         groups = range(TURNED // HALF)
         z_t = [[psum.tile([P, 2, 2, P], F32, name=f"z_t{u}{g}", tag=f"bank{4 + 2 * u + g}") for g in groups] for u in range(2)]
@@ -185,10 +194,13 @@ def tile_picked_devox_relu_p_kernel(
         for u in range(2):
             rounded.append([keep.tile([P, 2 * P * 2], BF16, name=f"rounded{u}{g}", align_bytes=64) for g in groups])
             for g in groups:
-                round_out = nc.vector.tensor_copy if (u, g) == (0, 1) else nc.scalar.copy
-                round_out(
-                    rounded[u][g][:].rearrange("r (b p e) -> r b p e", b=2, e=2), z_t[u][g][:].rearrange("r b e p -> r b p e")
-                )
+                to = rounded[u][g][:].rearrange("r (b p e) -> r b p e", b=2, e=2)
+                summed = z_t[u][g][:].rearrange("r b e p -> r b p e")
+                if (u, g) == (0, 1):
+                    nc.vector.tensor_copy(to[:, 1], summed[:, 1])
+                    nc.scalar.copy(to[:, 0], summed[:, 0])
+                else:
+                    nc.scalar.copy(to, summed)
         for lo, hi in RANGES:
             woven[lo] = keep.tile([P, (hi - lo) * PACK], BF16, name=f"woven{lo}", align_bytes=64)
             if lo >= TURNED:
@@ -204,7 +216,7 @@ def tile_picked_devox_relu_p_kernel(
                         words = rounded[u][b // 2][:].bitcast(F32)[:, (b % 2) * P : (b % 2 + 1) * P]
                         nc.tensor.transpose(back[:, u, at : at + P], words, ident[:])
                 nc.scalar.copy(woven[lo][:].bitcast(F32).rearrange("p (r u) -> p r u", u=2), back[:].rearrange("p u r -> p r u"))
-        late = []
+        left = []
         for lo, hi in RANGES:
             width = hi - lo
             zq = keep.tile([P, width], U32, name=f"zq{lo}", align_bytes=64)
@@ -222,53 +234,52 @@ def tile_picked_devox_relu_p_kernel(
                 stop=True,
             )
             if lo in VECTOR_RELU:
-                late.append((slice(lo, hi), y_acc))
+                left.append((slice(lo, hi), y_acc))
             else:
                 nc.scalar.activation(y[:, lo:hi], y_acc[:], RELU)
-        for cells, y_acc in late:
+        for cells, y_acc in left:
             nc.vector.tensor_scalar_max(y[:, cells], y_acc[:], 0.0)
 
+        halves = [slice(a * HALF, (a + 1) * HALF) for a in range(2)]
         plain = keep.tile([P, V], F32, name="plain")
         turned = []
         for a in range(2):
-            cols = slice(a * HALF, (a + 1) * HALF)
-            nc.scalar.activation(plain[:, cols], y[:].indirect(entries(pos_sb[0], a * HALF, (a + 1) * HALF)), COPY)
+            nc.scalar.activation(plain[:, halves[a]], y[:].indirect(entries(pos_sb[0], a * HALF, (a + 1) * HALF)), COPY)
             turned.append(psum.tile([P, 2, P], F32, name=f"turned{a}", tag=f"bank{(3, 1)[a]}"))
             for b in range(2):
                 nc.tensor.transpose(turned[a][:, b, :], plain[:, a * HALF + b * P : a * HALF + (b + 1) * P], ident[:])
-        terms = [keep.tile([P, V], F32, name=f"term{d}") for d in range(3)]
-        both = [psum.tile([P, 2, P], F32, name=f"both{a}", tag=f"bank{(2, 7)[a]}") for a in range(2)]
-        for d, width in ((0, V), (1, HALF), (2, HALF)):
-            for lo in range(0, V, width):
-                cols = slice(lo, lo + width)
-                nc.vector.tensor_tensor(terms[d][:, cols], y[:].indirect(entries(pos_sb[d + 1], lo, lo + width)), gate_sb[:, d, cols], MULT)
-                if d < 2:
-                    for b in range(lo // P, (lo + width) // P):
-                        nc.tensor.matmul(
-                            both[b // 2][:, b % 2, :],
-                            terms[d][:, b * P : (b + 1) * P],
-                            ident[:],
-                            start=(d == 0 and b % 2 == 0),
-                            stop=(d == 1 and b % 2 == 1),
-                            is_transpose=True,
-                        )
-        sums = [psum.tile([P, hi - lo], F32, name=f"sum{lo}", tag=f"bank{(0, 4, 5)[i]}") for i, (lo, hi) in enumerate(OUT_PARTS)]
-
-        def turn_back(source, b, start, stop):
-            part = max(0, b - 1)
-            at = b * P - OUT_PARTS[part][0]
-            nc.tensor.matmul(sums[part][:, at : at + P], source, ident[:], start=start, stop=stop, is_transpose=True)
-
+        terms = {d: keep.tile([P, V], F32, name=f"term{d}") for d in range(1, D)}
+        carried_terms = ((1, 2), (1,))
+        early_sum = [psum.tile([P, 2, P], F32, name=f"early_sum{a}", tag=f"bank{(2, 7)[a]}") for a in range(2)]
+        for d, a in ((1, 0), (2, 0), (1, 1), (2, 1), (3, 1), (3, 0)):
+            window = y[:].indirect(entries(pos_sb[d], a * HALF, (a + 1) * HALF))
+            nc.vector.tensor_tensor(terms[d][:, halves[a]], window, gate_sb[:, d - 1, halves[a]], MULT)
+            if d in carried_terms[a]:
+                for b in range(2):
+                    nc.tensor.matmul(
+                        early_sum[a][:, b, :],
+                        terms[d][:, a * HALF + b * P : a * HALF + (b + 1) * P],
+                        ident[:],
+                        start=(d == carried_terms[a][0] and b == 0),
+                        stop=(d == carried_terms[a][-1] and b == 1),
+                        is_transpose=True,
+                    )
+        sums = [psum.tile([P, 2, P], F32, name=f"sum{a}", tag=f"bank{(0, 4)[a]}") for a in range(2)]
         for b in range(V // P):
             weighted = keep.tile([P, P], F32, name=f"weighted{b}")
             nc.scalar.activation(weighted[:], turned[b // 2][:, b % 2, :], COPY, scale=gate_t[:, b : b + 1])
-            turn_back(weighted[:], b, b != 1, False)
+            nc.tensor.matmul(sums[b // 2][:, b % 2, :], weighted[:], ident[:], start=(b % 2 == 0), stop=False, is_transpose=True)
         for a in range(2):
             carried = keep.tile([P, 2, P], F32, name=f"carried{a}")
-            nc.scalar.copy(carried[:], both[a][:])
+            nc.scalar.copy(carried[:], early_sum[a][:])
             for b in range(2):
-                turn_back(carried[:, b, :], 2 * a + b, False, 2 * a + b != 0)
-        for (lo, hi), part_sum, queue in zip(OUT_PARTS, sums, (nc.sync, nc.scalar, nc.sync)):
+                nc.tensor.matmul(sums[a][:, b, :], carried[:, b, :], ident[:], start=False, stop=(b == 1), is_transpose=True)
+        late_sum = keep.tile([P, HALF], F32, name="late_sum")
+        nc.vector.tensor_tensor(late_sum[:], terms[2][:, halves[1]], terms[3][:, halves[1]], ADD)
+        for (lo, hi), queue in zip(OUT_PARTS, (nc.sync, nc.scalar, nc.sync)):
+            a = lo // HALF
+            cols = slice(lo - a * HALF, hi - a * HALF)
+            late = terms[3][:, halves[0]] if a == 0 else late_sum[:]
             res = keep.tile([P, hi - lo], F32, name=f"res{lo}")
-            nc.vector.tensor_tensor(res[:], part_sum[:], terms[2][:, lo:hi], ADD)
+            nc.vector.tensor_tensor(res[:], sums[a][:].rearrange("p b v -> p (b v)")[:, cols], late[:, cols], ADD)
             queue.dma_start(out[:, lo:hi], res[:])

@@ -24,11 +24,11 @@ PER_COLUMN = 16
 HALF = S // 2
 W1_SPLIT = 104
 WORD_PIECES = ((0, 128), (128, 256), (256, 512))
-RANGES = ((512, 768), (768, 1024), (0, 256), (256, 384), (384, 512))
+RANGES = ((512, 768), (768, 1024), (0, 256), (256, 384), (384, 448), (448, 512))
 TURNED = 512
 FIRST = 128
-Y_BANKS = {512: 7, 768: 0, 0: 4, 256: 5, 384: 6}
-VECTOR_RELU = (256, 384)
+Y_BANKS = {512: 7, 768: 0, 0: 4, 256: 5, 384: 6, 448: 3}
+VECTOR_RELU = (256, 448)
 ADDS = ((0, 512, 1024), (1, 512, 1024), (2, 512, 1024), (3, 512, 768), (3, 768, 1024))
 OUT_PARTS = ((0, 256), (256, 384), (384, 512))
 
@@ -92,7 +92,7 @@ def tile_picked_devox_relu_p_kernel(
             a = lo // HALF
             nc.vector.tensor_copy(xw[a][:, lo - a * HALF : hi - a * HALF], xw_all[:].indirect(entries(offs_sb, lo, hi)))
 
-        h_first = keep.tile([P, 2, FIRST], F32, name="h_first")
+        h_first = [keep.tile([P, FIRST], F32, name=f"h_first{e}") for e in range(2)]
         h_rest = [keep.tile([P, 2 * S - FIRST], F32, name=f"h_rest{e}") for e in range(2)]
         later = S - FIRST
 
@@ -122,10 +122,10 @@ def tile_picked_devox_relu_p_kernel(
             else:
                 nc.scalar.activation(window, values, COPY)
 
-        first = psum.tile([P, 2, FIRST], F32, name="first", tag="bank0")
         for e in range(2):
-            product(first[:, e, :], e, 0, FIRST)
-        relu(1, h_first[:], first[:])
+            first = psum.tile([P, FIRST], F32, name=f"first{e}", tag=f"bank{(4, 0)[e]}")
+            product(first[:], e, 0, FIRST)
+            relu(1, h_first[e][:], first[:])
         for e in range(2):
             second = psum.tile([P, FIRST], F32, name=f"second{e}", tag=f"bank{(3, 1)[e]}")
             product(second[:], e, FIRST, HALF)
@@ -157,15 +157,14 @@ def tile_picked_devox_relu_p_kernel(
             nc.sync.dma_start(gate_t[:], gate[0, 0, :].rearrange("(b p) -> p b", p=P))
         nc.sync.dma_start(gate_sb[:], gate[1:].rearrange("d p v -> p d v"))
 
-        scatter(0, 0, FIRST, h_first[:, 0, :])
-        relu(0, h_rest[0][:, FIRST:later], mixed[0][:, :HALF])
-        relu(0, h_rest[0][:, later : later + HALF], mixed[0][:, HALF:])
+        scatter(0, 0, FIRST, h_first[0][:])
+        relu(0, h_rest[0][:, FIRST : FIRST + S], mixed[0][:])
+        relu(0, h_rest[0][:, FIRST + S :], last[0][:])
         scatter(0, FIRST, S, h_rest[0][:, :later])
-        scatter(1, 0, FIRST, h_first[:, 1, :])
+        scatter(1, 0, FIRST, h_first[1][:])
         relu(1, h_rest[1][:, later : later + HALF], mixed[1][:, HALF:])
         relu(1, h_rest[1][:, FIRST:later], mixed[1][:, :HALF])
         scatter(3, 0, HALF, h_rest[1][:, later : later + HALF])
-        relu(1, h_rest[0][:, FIRST + S :], last[0][:])
         relu(1, h_rest[1][:, FIRST + S :], last[1][:])
         scatter(2, 0, S, h_rest[0][:, later:])
         scatter(1, FIRST, S, h_rest[1][:, :later])
@@ -209,13 +208,18 @@ def tile_picked_devox_relu_p_kernel(
                     z[:, :, lo - TURNED : hi - TURNED].rearrange("p t r -> p r t"),
                 )
             else:
-                back = psum.tile([P, 2, hi - lo], F32, name=f"back{lo}", tag=f"bank{max(0, lo // P - 1)}")
-                for u in range(2):
-                    for b in range(lo // P, hi // P):
-                        at = b * P - lo
-                        words = rounded[u][b // 2][:].bitcast(F32)[:, (b % 2) * P : (b % 2 + 1) * P]
-                        nc.tensor.transpose(back[:, u, at : at + P], words, ident[:])
-                nc.scalar.copy(woven[lo][:].bitcast(F32).rearrange("p (r u) -> p r u", u=2), back[:].rearrange("p u r -> p r u"))
+                if lo % P == 0:
+                    start, width = lo, max(P, hi - lo)
+                    back = psum.tile([P, 2, width], F32, name=f"back{lo}", tag=f"bank{max(0, lo // P - 1)}")
+                    for u in range(2):
+                        for b in range(lo // P, (lo + width) // P):
+                            at = b * P - lo
+                            words = rounded[u][b // 2][:].bitcast(F32)[:, (b % 2) * P : (b % 2 + 1) * P]
+                            nc.tensor.transpose(back[:, u, at : at + P], words, ident[:])
+                nc.scalar.copy(
+                    woven[lo][:].bitcast(F32).rearrange("p (r u) -> p r u", u=2),
+                    back[:, :, lo - start : hi - start].rearrange("p u r -> p r u"),
+                )
         left = []
         for lo, hi in RANGES:
             width = hi - lo
@@ -240,46 +244,47 @@ def tile_picked_devox_relu_p_kernel(
         for cells, y_acc in left:
             nc.vector.tensor_scalar_max(y[:, cells], y_acc[:], 0.0)
 
-        halves = [slice(a * HALF, (a + 1) * HALF) for a in range(2)]
         plain = keep.tile([P, V], F32, name="plain")
         turned = []
         for a in range(2):
-            nc.scalar.activation(plain[:, halves[a]], y[:].indirect(entries(pos_sb[0], a * HALF, (a + 1) * HALF)), COPY)
+            cols = slice(a * HALF, (a + 1) * HALF)
+            nc.scalar.activation(plain[:, cols], y[:].indirect(entries(pos_sb[0], a * HALF, (a + 1) * HALF)), COPY)
             turned.append(psum.tile([P, 2, P], F32, name=f"turned{a}", tag=f"bank{(3, 1)[a]}"))
             for b in range(2):
                 nc.tensor.transpose(turned[a][:, b, :], plain[:, a * HALF + b * P : a * HALF + (b + 1) * P], ident[:])
-        terms = {d: keep.tile([P, V], F32, name=f"term{d}") for d in range(1, D)}
-        carried_terms = ((1, 2), (1,))
-        early_sum = [psum.tile([P, 2, P], F32, name=f"early_sum{a}", tag=f"bank{(2, 7)[a]}") for a in range(2)]
-        for d, a in ((1, 0), (2, 0), (1, 1), (2, 1), (3, 1), (3, 0)):
-            window = y[:].indirect(entries(pos_sb[d], a * HALF, (a + 1) * HALF))
-            nc.vector.tensor_tensor(terms[d][:, halves[a]], window, gate_sb[:, d - 1, halves[a]], MULT)
-            if d in carried_terms[a]:
-                for b in range(2):
-                    nc.tensor.matmul(
-                        early_sum[a][:, b, :],
-                        terms[d][:, a * HALF + b * P : a * HALF + (b + 1) * P],
-                        ident[:],
-                        start=(d == carried_terms[a][0] and b == 0),
-                        stop=(d == carried_terms[a][-1] and b == 1),
-                        is_transpose=True,
-                    )
-        sums = [psum.tile([P, 2, P], F32, name=f"sum{a}", tag=f"bank{(0, 4)[a]}") for a in range(2)]
+        terms = [keep.tile([P, V], F32, name=f"term{d}") for d in range(3)]
+        both = [psum.tile([P, 2, P], F32, name=f"both{a}", tag=f"bank{(2, 7)[a]}") for a in range(2)]
+        for d, width in ((0, V), (1, HALF), (2, HALF)):
+            for lo in range(0, V, width):
+                cols = slice(lo, lo + width)
+                nc.vector.tensor_tensor(terms[d][:, cols], y[:].indirect(entries(pos_sb[d + 1], lo, lo + width)), gate_sb[:, d, cols], MULT)
+                if d < 2:
+                    for b in range(lo // P, (lo + width) // P):
+                        nc.tensor.matmul(
+                            both[b // 2][:, b % 2, :],
+                            terms[d][:, b * P : (b + 1) * P],
+                            ident[:],
+                            start=(d == 0 and b % 2 == 0),
+                            stop=(d == 1 and b % 2 == 1),
+                            is_transpose=True,
+                        )
+        sums = [psum.tile([P, hi - lo], F32, name=f"sum{lo}", tag=f"bank{(0, 4, 5)[i]}") for i, (lo, hi) in enumerate(OUT_PARTS)]
+
+        def turn_back(source, b, start, stop):
+            part = max(0, b - 1)
+            at = b * P - OUT_PARTS[part][0]
+            nc.tensor.matmul(sums[part][:, at : at + P], source, ident[:], start=start, stop=stop, is_transpose=True)
+
         for b in range(V // P):
             weighted = keep.tile([P, P], F32, name=f"weighted{b}")
             nc.scalar.activation(weighted[:], turned[b // 2][:, b % 2, :], COPY, scale=gate_t[:, b : b + 1])
-            nc.tensor.matmul(sums[b // 2][:, b % 2, :], weighted[:], ident[:], start=(b % 2 == 0), stop=False, is_transpose=True)
+            turn_back(weighted[:], b, b != 1, False)
         for a in range(2):
             carried = keep.tile([P, 2, P], F32, name=f"carried{a}")
-            nc.scalar.copy(carried[:], early_sum[a][:])
+            nc.scalar.copy(carried[:], both[a][:])
             for b in range(2):
-                nc.tensor.matmul(sums[a][:, b, :], carried[:, b, :], ident[:], start=False, stop=(b == 1), is_transpose=True)
-        late_sum = keep.tile([P, HALF], F32, name="late_sum")
-        nc.vector.tensor_tensor(late_sum[:], terms[2][:, halves[1]], terms[3][:, halves[1]], ADD)
-        for (lo, hi), queue in zip(OUT_PARTS, (nc.sync, nc.scalar, nc.sync)):
-            a = lo // HALF
-            cols = slice(lo - a * HALF, hi - a * HALF)
-            late = terms[3][:, halves[0]] if a == 0 else late_sum[:]
+                turn_back(carried[:, b, :], 2 * a + b, False, 2 * a + b != 0)
+        for (lo, hi), part_sum, queue in zip(OUT_PARTS, sums, (nc.sync, nc.scalar, nc.sync)):
             res = keep.tile([P, hi - lo], F32, name=f"res{lo}")
-            nc.vector.tensor_tensor(res[:], sums[a][:].rearrange("p b v -> p (b v)")[:, cols], late[:, cols], ADD)
+            nc.vector.tensor_tensor(res[:], part_sum[:], terms[2][:, lo:hi], ADD)
             queue.dma_start(out[:, lo:hi], res[:])

from contextlib import ExitStack

import concourse.mybir as mybir
from concourse.masks import make_identity

K, T, S, D, V, H, N, U = 512, 2048, 512, 4, 512, 512, 128, 1024
FLOPS = 2 * K * H * S + 2 * H * N * U

F32 = mybir.dt.float32
BF16 = mybir.dt.bfloat16
I32 = mybir.dt.int32
U32 = mybir.dt.uint32
U16 = mybir.dt.uint16
U8 = mybir.dt.uint8
FP8X4 = mybir.dt.float8_e4m3fn_x4
ADD = mybir.AluOpType.add
MULT = mybir.AluOpType.mult
RELU = mybir.ActivationFunctionType.Relu
COPY = mybir.ActivationFunctionType.Copy

P = 128
PACK = 4
PER_COLUMN = 16
HALF = S // 2
W1_SPLIT = 104
WORD_PIECES = ((0, 128), (128, 256), (256, 512))
RANGES = ((512, 768), (768, 1024), (0, 256), (256, 384), (384, 448), (448, 512))
TURNED = 512
FIRST = 128
Y_BANKS = {512: 7, 768: 0, 0: 4, 256: 5, 384: 6, 448: 3}
VECTOR_RELU = (256, 448)
ADDS = ((0, 512, 1024), (1, 512, 1024), (2, 512, 1024), (3, 512, 768), (3, 768, 1024))
OUT_PARTS = ((0, 256), (256, 384), (384, 512))


def entries(list_tile, lo, hi):
    return list_tile[:, lo // PER_COLUMN : hi // PER_COLUMN]


def tile_picked_devox_relu_p_kernel(
    tc, x_words, x_scales, w1, w2_words, w2_scales, gate, emb, offs, cell, pos1, pos2, pos3, pos4, out
):
    nc = tc.nc
    with ExitStack() as ctx:
        keep = ctx.enter_context(tc.tile_pool(name="keep", bufs=1))
        psum = ctx.enter_context(tc.psum_pool(name="psum", bufs=1))

        offs_sb = keep.tile([P, S // PER_COLUMN], U16, name="offs_sb")
        cell_sb = keep.tile([P, S // PER_COLUMN], U16, name="cell_sb")
        pos_sb = [keep.tile([P, V // PER_COLUMN], U16, name=f"pos_sb{d}") for d in range(D)]
        xs_all = keep.tile([P, T], U8, name="xs_all", align_bytes=64)
        xw_all = keep.tile([P, T], U32, name="xw_all", tag="xw_all", align_bytes=64)
        w1_raw = keep.tile([P, PACK, H], F32, name="w1_raw", tag="w1_raw", align_bytes=64)
        ident = keep.tile([P, P], F32, name="ident")
        up = [keep.tile([P, U], F32, name=f"up{t}") for t in range(PACK)]

        nc.gpsimd.memset(xs_all[:].bitcast(I32), 0)
        nc.vector.memset(up[0][:].bitcast(I32), 0)
        nc.scalar.copy(up[1][:], up[0][:])
        for t in (2, 3):
            nc.vector.tensor_copy(up[t][:], up[0][:])

        w1_rows = w1.rearrange("(p j) c -> p j c", j=PACK)
        nc.sync.dma_start(offs_sb[:], offs)
        nc.scalar.dma_start(w1_raw[:, :1, :], w1_rows[:, :1, :])
        nc.sync.dma_start(cell_sb[:], cell)
        nc.sync.dma_start(xs_all[0:P:8, :].bitcast(I32), x_scales[0].bitcast(I32))
        nc.sync.dma_start(w1_raw[:, 1:, :], w1_rows[:, 1:, :])
        nc.sync.dma_start(xw_all[:].bitcast(I32), x_words[0].rearrange("p n t -> p (n t)").bitcast(I32))
        for d, pos in enumerate((pos1, pos2, pos3, pos4)):
            nc.sync.dma_start(pos_sb[d][:], pos)
        make_identity(nc, ident[:])

        xs_spread = keep.tile([P, S], U8, name="xs_spread", tag="xs_spread", align_bytes=64)
        xs = keep.tile([P, S], U8, name="xs", tag="xs", align_bytes=64)
        nc.vector.tensor_copy(xs_spread[:], xs_all[:].indirect(offs_sb[:]))
        nc.vector.tensor_copy(xs[:].bitcast(I32), xs_spread[:].bitcast(I32))
        for r in range(1, 4):
            nc.scalar.dma_start(xs[r:P:32, :].bitcast(I32), xs[8 * r : P : 32, :].bitcast(I32))

        w1_bf = keep.tile([P, PACK * P * PACK], BF16, name="w1_bf", tag="w1_bf", align_bytes=64)
        w1_to = w1_bf[:].rearrange("p (t m j) -> p m j t", t=PACK, j=PACK)
        w1_from = w1_raw[:].rearrange("p j (m t) -> p m j t", t=PACK)
        nc.vector.tensor_copy(w1_to[:, :W1_SPLIT], w1_from[:, :W1_SPLIT])
        nc.scalar.copy(w1_to[:, W1_SPLIT:], w1_from[:, W1_SPLIT:])
        w1q = keep.tile([P, H], U32, name="w1q", tag="w1q", align_bytes=64)
        w1s = keep.tile([P, H], U8, name="w1s", tag="w1s", align_bytes=64)
        nc.vector.quantize_mx(out=w1q[:].bitcast(FP8X4), scales=w1s[:], in_=w1_bf[:])

        xw = [keep.tile([P, HALF], U32, name=f"xw{a}", tag=f"xw{a}", align_bytes=64) for a in range(2)]
        for lo, hi in WORD_PIECES:
            a = lo // HALF
            nc.vector.tensor_copy(xw[a][:, lo - a * HALF : hi - a * HALF], xw_all[:].indirect(entries(offs_sb, lo, hi)))

        h_first = [keep.tile([P, FIRST], F32, name=f"h_first{e}") for e in range(2)]
        h_rest = [keep.tile([P, 2 * S - FIRST], F32, name=f"h_rest{e}") for e in range(2)]
        later = S - FIRST

        def product(to, t, lo, hi):
            a = lo // HALF
            plane_cols = slice(t * P, (t + 1) * P)
            nc.tensor.matmul_mx(
                out=to,
                lhsT=w1q[:, plane_cols].bitcast(FP8X4),
                lhsT_scale=w1s[:, plane_cols],
                rhs=xw[a][:, lo - a * HALF : hi - a * HALF].bitcast(FP8X4),
                rhs_scale=xs[:, lo:hi],
                start=True,
                stop=True,
            )

        def relu(e, to, acc):
            if e == 0:
                nc.vector.tensor_scalar_max(to, acc, 0.0)
            else:
                nc.scalar.activation(to, acc, RELU)

        def scatter(t, lo, hi, values):
            window = up[t][:].indirect(entries(cell_sb, lo, hi))
            if t % 2 == 0:
                nc.vector.tensor_copy(window, values)
            else:
                nc.scalar.activation(window, values, COPY)

        for e in range(2):
            first = psum.tile([P, FIRST], F32, name=f"first{e}", tag=f"bank{(4, 0)[e]}")
            product(first[:], e, 0, FIRST)
            relu(1, h_first[e][:], first[:])
        for e in range(2):
            second = psum.tile([P, FIRST], F32, name=f"second{e}", tag=f"bank{(3, 1)[e]}")
            product(second[:], e, FIRST, HALF)
            relu(e, h_rest[e][:, :FIRST], second[:])
        mixed = [psum.tile([P, S], F32, name=f"mixed{e}", tag=f"bank{(2, 0)[e]}") for e in range(2)]
        last = [psum.tile([P, HALF], F32, name=f"last{e}", tag=f"bank{(3, 1)[e]}") for e in range(2)]
        product(mixed[0][:, HALF:], 2, 0, HALF)
        product(mixed[0][:, :HALF], 0, HALF, S)
        product(mixed[1][:, HALF:], 3, 0, HALF)
        product(mixed[1][:, :HALF], 1, HALF, S)
        for e in range(2):
            product(last[e][:], 2 + e, HALF, S)

        emb_rows = emb.rearrange("(p t) r -> p t r", t=PACK)
        emb_sb = []
        for u, used_up in enumerate(("xw_all", "xw0")):
            emb_sb.append(keep.tile([P, 2, U], F32, name=f"emb_sb{u}", tag=used_up, align_bytes=64))
            nc.sync.dma_start(emb_sb[u][:], emb_rows[:, 2 * u : 2 * u + 2, :])

        w2w = keep.tile([P, N], U32, name="w2w", tag="w1q", align_bytes=64)
        w2s = keep.tile([P, N], U8, name="w2s", tag="xs", align_bytes=64)
        gate_sb = keep.tile([P, D - 1, V], F32, name="gate_sb", tag="xw1", align_bytes=64)
        gate_t = keep.tile([P, V // P], F32, name="gate_t", tag="w1s", align_bytes=64)
        nc.gpsimd.memset(w2s[:].bitcast(I32), 0)
        nc.sync.dma_start(w2w[:].bitcast(I32), w2_words[0].rearrange("p n t -> p (n t)").bitcast(I32))
        for q in range(4):
            nc.sync.dma_start(w2s[32 * q : 32 * q + 4, :].bitcast(I32), w2_scales[0][4 * q : 4 * q + 4, :].bitcast(I32))
        with nc.allow_non_contiguous_dma(reason="one gate weight a partition"):
            nc.sync.dma_start(gate_t[:], gate[0, 0, :].rearrange("(b p) -> p b", p=P))
        nc.sync.dma_start(gate_sb[:], gate[1:].rearrange("d p v -> p d v"))

        scatter(0, 0, FIRST, h_first[0][:])
        relu(0, h_rest[0][:, FIRST : FIRST + S], mixed[0][:])
        relu(0, h_rest[0][:, FIRST + S :], last[0][:])
        scatter(0, FIRST, S, h_rest[0][:, :later])
        scatter(1, 0, FIRST, h_first[1][:])
        relu(1, h_rest[1][:, later : later + HALF], mixed[1][:, HALF:])
        relu(1, h_rest[1][:, FIRST:later], mixed[1][:, :HALF])
        scatter(3, 0, HALF, h_rest[1][:, later : later + HALF])
        relu(1, h_rest[1][:, FIRST + S :], last[1][:])
        scatter(2, 0, S, h_rest[0][:, later:])
        scatter(1, FIRST, S, h_rest[1][:, :later])
        scatter(3, HALF, S, h_rest[1][:, later + HALF :])

        groups = range(TURNED // HALF)
        z_t = [[psum.tile([P, 2, 2, P], F32, name=f"z_t{u}{g}", tag=f"bank{4 + 2 * u + g}") for g in groups] for u in range(2)]
        for u in range(2):
            sources = [emb_sb[u][:, e, :] for e in range(2)] + [up[2 * u + e][:] for e in range(2)]
            for i, source in enumerate(sources):
                for g in groups:
                    for b in range(2):
                        cells = slice(g * HALF + b * P, g * HALF + (b + 1) * P)
                        first, final = (i, b) == (0, 0), (i, b) == (3, 1)
                        nc.tensor.matmul(
                            z_t[u][g][:, b, i % 2, :], source[:, cells], ident[:], start=first, stop=final, is_transpose=True
                        )
        z = keep.tile([P, PACK, U - TURNED], F32, name="z")
        for t, lo, hi in ADDS:
            engine = nc.gpsimd if t < 2 else nc.vector
            engine.tensor_tensor(z[:, t, lo - TURNED : hi - TURNED], up[t][:, lo:hi], emb_sb[t // 2][:, t % 2, lo:hi], ADD)

        y = keep.tile([P, U], F32, name="y")
        woven = {}
        rounded = []
        for u in range(2):
            rounded.append([keep.tile([P, 2 * P * 2], BF16, name=f"rounded{u}{g}", align_bytes=64) for g in groups])
            for g in groups:
                to = rounded[u][g][:].rearrange("r (b p e) -> r b p e", b=2, e=2)
                summed = z_t[u][g][:].rearrange("r b e p -> r b p e")
                if (u, g) == (0, 1):
                    nc.vector.tensor_copy(to[:, 1], summed[:, 1])
                    nc.scalar.copy(to[:, 0], summed[:, 0])
                else:
                    nc.scalar.copy(to, summed)
        for lo, hi in RANGES:
            woven[lo] = keep.tile([P, (hi - lo) * PACK], BF16, name=f"woven{lo}", align_bytes=64)
            if lo >= TURNED:
                nc.vector.tensor_copy(
                    woven[lo][:].rearrange("p (r t) -> p r t", t=PACK),
                    z[:, :, lo - TURNED : hi - TURNED].rearrange("p t r -> p r t"),
                )
            else:
                if lo % P == 0:
                    start, width = lo, max(P, hi - lo)
                    back = psum.tile([P, 2, width], F32, name=f"back{lo}", tag=f"bank{max(0, lo // P - 1)}")
                    for u in range(2):
                        for b in range(lo // P, (lo + width) // P):
                            at = b * P - lo
                            words = rounded[u][b // 2][:].bitcast(F32)[:, (b % 2) * P : (b % 2 + 1) * P]
                            nc.tensor.transpose(back[:, u, at : at + P], words, ident[:])
                nc.scalar.copy(
                    woven[lo][:].bitcast(F32).rearrange("p (r u) -> p r u", u=2),
                    back[:, :, lo - start : hi - start].rearrange("p u r -> p r u"),
                )
        left = []
        for lo, hi in RANGES:
            width = hi - lo
            zq = keep.tile([P, width], U32, name=f"zq{lo}", align_bytes=64)
            zs = keep.tile([P, width], U8, name=f"zs{lo}", align_bytes=64)
            nc.vector.quantize_mx(out=zq[:].bitcast(FP8X4), scales=zs[:], in_=woven[lo][:])
            bank = Y_BANKS[lo]
            y_acc = psum.tile([P, width], F32, name=f"yacc{lo}", tag=f"bank{bank}")
            nc.tensor.matmul_mx(
                out=y_acc[:],
                lhsT=w2w[:].bitcast(FP8X4),
                lhsT_scale=w2s[:],
                rhs=zq[:].bitcast(FP8X4),
                rhs_scale=zs[:],
                start=True,
                stop=True,
            )
            if lo in VECTOR_RELU:
                left.append((slice(lo, hi), y_acc))
            else:
                nc.scalar.activation(y[:, lo:hi], y_acc[:], RELU)
        for cells, y_acc in left:
            nc.vector.tensor_scalar_max(y[:, cells], y_acc[:], 0.0)

        plain = keep.tile([P, V], F32, name="plain")
        turned = []
        for a in range(2):
            cols = slice(a * HALF, (a + 1) * HALF)
            nc.scalar.activation(plain[:, cols], y[:].indirect(entries(pos_sb[0], a * HALF, (a + 1) * HALF)), COPY)
            turned.append(psum.tile([P, 2, P], F32, name=f"turned{a}", tag=f"bank{(3, 1)[a]}"))
            for b in range(2):
                nc.tensor.transpose(turned[a][:, b, :], plain[:, a * HALF + b * P : a * HALF + (b + 1) * P], ident[:])
        terms = [keep.tile([P, V], F32, name=f"term{d}") for d in range(3)]
        both = [psum.tile([P, 2, P], F32, name=f"both{a}", tag=f"bank{(2, 7)[a]}") for a in range(2)]
        for d, width in ((0, V), (1, HALF), (2, HALF)):
            for lo in range(0, V, width):
                cols = slice(lo, lo + width)
                nc.vector.tensor_tensor(terms[d][:, cols], y[:].indirect(entries(pos_sb[d + 1], lo, lo + width)), gate_sb[:, d, cols], MULT)
                if d < 2:
                    for b in range(lo // P, (lo + width) // P):
                        nc.tensor.matmul(
                            both[b // 2][:, b % 2, :],
                            terms[d][:, b * P : (b + 1) * P],
                            ident[:],
                            start=(d == 0 and b % 2 == 0),
                            stop=(d == 1 and b % 2 == 1),
                            is_transpose=True,
                        )
        sums = [psum.tile([P, hi - lo], F32, name=f"sum{lo}", tag=f"bank{(0, 4, 5)[i]}") for i, (lo, hi) in enumerate(OUT_PARTS)]

        def turn_back(source, b, start, stop):
            part = max(0, b - 1)
            at = b * P - OUT_PARTS[part][0]
            nc.tensor.matmul(sums[part][:, at : at + P], source, ident[:], start=start, stop=stop, is_transpose=True)

        for b in range(V // P):
            weighted = keep.tile([P, P], F32, name=f"weighted{b}")
            nc.scalar.activation(weighted[:], turned[b // 2][:, b % 2, :], COPY, scale=gate_t[:, b : b + 1])
            turn_back(weighted[:], b, b != 1, False)
        for a in range(2):
            carried = keep.tile([P, 2, P], F32, name=f"carried{a}")
            nc.scalar.copy(carried[:], both[a][:])
            for b in range(2):
                turn_back(carried[:, b, :], 2 * a + b, False, 2 * a + b != 0)
        for (lo, hi), part_sum, queue in zip(OUT_PARTS, sums, (nc.sync, nc.scalar, nc.sync)):
            res = keep.tile([P, hi - lo], F32, name=f"res{lo}")
            nc.vector.tensor_tensor(res[:], part_sum[:], terms[2][:, lo:hi], ADD)
            queue.dma_start(out[:, lo:hi], res[:])
